import numpy as np
import ml_dtypes


def mxq(x, axis, fmt="e4m3"):
    dtype, down = {"e4m3": (ml_dtypes.float8_e4m3fn, 7), "e5m2": (ml_dtypes.float8_e5m2, 14)}[fmt]
    v = np.moveaxis(np.asarray(x, np.float32).astype(ml_dtypes.bfloat16).astype(np.float64), axis, -1)
    blocks = v.reshape(v.shape[:-1] + (-1, 32))
    amax = np.abs(blocks).max(-1, keepdims=True)
    byte = np.maximum(np.where(amax > 0, np.frexp(amax)[1] - 1 + 127, 0) - down, 1)
    scale = np.exp2(byte - 127.0)
    codes = (blocks / scale).astype(np.float32).astype(dtype).astype(np.float64)
    return np.moveaxis((codes * scale).reshape(v.shape), -1, axis)


WIDE = False


def mx_kscale(k):
    if not WIDE:
        return np.ones(k)
    levels = np.array([10, -10, 5, -5, 0])
    if k % 512:
        return np.exp2(np.random.permutation(np.resize(levels, k // 32))).repeat(32)
    a = np.empty((k // 512, 16))
    for p in range(k // 512):
        a[p, :8] = np.random.permutation(np.resize(levels, 8))
        for g in range(8):
            far = levels[np.abs(levels - a[p, g]) >= 10]
            a[p, g + 8] = far[np.random.randint(len(far))]
    return np.exp2(a.ravel()).repeat(32)


def f64(x):
    return np.asarray(x).astype(np.float64)


def striped(idx):
    return np.tile(idx.reshape(-1, 16).T, (8, 1)).astype(np.uint16)


def unstriped(offs):
    return offs[:16].T.reshape(-1).astype(np.int64)


E2M1 = np.array([0.0, 0.5, 1.0, 1.5, 2.0, 3.0, 4.0, 6.0, -0.0, -0.5, -1.0, -1.5, -2.0, -3.0, -4.0, -6.0])


def pack_weight(w, fmt):
    k, n = w.shape
    w = f64(np.asarray(w, np.float32).astype(ml_dtypes.bfloat16)).reshape(k // 32, 32, n)
    amax = np.abs(w).max(1)
    if fmt == "e4m3":
        byte = np.frexp(amax)[1] - 1 + 127 - 7
    else:
        mant, ex = np.frexp(amax / 6.0)
        byte = np.where(mant > 0.5, ex, ex - 1) + 127
    byte = np.clip(np.where(amax > 0, byte, 1), 1, 254)
    scaled = (w * np.exp2(127.0 - byte)[:, None, :]).reshape(k, n).astype(np.float32)
    by_word = np.ascontiguousarray(scaled.reshape(k // 512, 128, 4, n).transpose(0, 1, 3, 2))
    if fmt == "e4m3":
        words = by_word.astype(ml_dtypes.float8_e4m3fn).view(np.uint8)
    else:
        c = by_word.astype(ml_dtypes.float4_e2m1fn).view(np.uint8) & 0xF
        words = (c[..., 0::2] | (c[..., 1::2] << 4)).reshape(k // 512, 128, 2 * n)
    return np.ascontiguousarray(words), np.ascontiguousarray(byte.astype(np.uint8).reshape(k // 512, 16, n))


def unpack_weight(words, scales, fmt):
    g, _, n = scales.shape
    words = np.ascontiguousarray(words).reshape(g, 128, n, -1)
    if fmt == "e4m3":
        vals = words.view(ml_dtypes.float8_e4m3fn).astype(np.float64)
    else:
        nib = np.empty((g, 128, n, 4), np.uint8)
        nib[..., 0::2] = words & 0xF
        nib[..., 1::2] = words >> 4
        vals = E2M1[nib]
    vals = vals * np.repeat(np.exp2(scales.astype(np.float64) - 127.0), 8, axis=1)[..., None]
    return vals.transpose(0, 1, 3, 2).reshape(g * 512, n)


def gelu(v):
    return 0.5 * v * (1.0 + np.tanh(np.sqrt(2.0 / np.pi) * (v + 0.044715 * v**3)))


K, K2, H, N, T, T2, S = 1024, 512, 1024, 512, 2048, 4096, 1024

def setup_inputs():
    n = np.random.standard_normal
    s = mx_kscale(K)[:, None]
    s2 = mx_kscale(K2)[:, None]
    u = mx_kscale(H)[:, None]
    tab_words, tab_scales = pack_weight(n((K, T)) * s, "e4m3")
    tab2_words, tab2_scales = pack_weight(n((K2, T2)) * s2, "e4m3")
    wv_words, wv_scales = pack_weight(n((K2, H)) / np.sqrt(K2) / s2 * u.T, "e2m1")
    return {
        "tab_words": tab_words, "tab_scales": tab_scales,
        "offs": striped(np.random.permutation(T)[:S]),
        "tab2_words": tab2_words, "tab2_scales": tab2_scales,
        "offs2": striped(np.random.permutation(T2)[:S]),
        "wg": (1.5 * n((K, H)) / np.sqrt(K) / s).astype(np.float32),
        "bg": (0.5 * n(H)).astype(np.float32),
        "wv_words": wv_words, "wv_scales": wv_scales,
        "wo": (2.0 * n((H, N)) / np.sqrt(H) / u).astype(np.float32),
        "bo": (0.5 * n(N)).astype(np.float32),
    }

def reference(tab_words, tab_scales, offs, tab2_words, tab2_scales, offs2,
              wg, bg, wv_words, wv_scales, wo, bo):
    v = unpack_weight(tab_words, tab_scales, "e4m3")[:, unstriped(offs)]
    v2 = unpack_weight(tab2_words, tab2_scales, "e4m3")[:, unstriped(offs2)]
    wv = unpack_weight(wv_words, wv_scales, "e2m1")
    g = (mxq(f64(wg), 0, "e4m3").T @ v) + f64(bg)[:, None]
    a = wv.T @ v2
    h = a * (1.0 / (1.0 + np.exp(-g)))
    y = mxq(f64(wo), 0, "e4m3").T @ mxq(h, 0, "e4m3")
    return y + f64(bo)[:, None]

@@ -1,0 +1,215 @@
+from contextlib import ExitStack
+
+import concourse.mybir as mybir
+
+K, K2, H, N, T, T2, S = 1024, 512, 1024, 512, 2048, 4096, 1024
+FLOPS = 2 * S * (K * H + K2 * H + H * N)
+
+F32 = mybir.dt.float32
+BF16 = mybir.dt.bfloat16
+I32 = mybir.dt.int32
+U32 = mybir.dt.uint32
+U16 = mybir.dt.uint16
+U8 = mybir.dt.uint8
+FP8X4 = mybir.dt.float8_e4m3fn_x4
+FP4X4 = mybir.dt.float4_e2m1fn_x4
+ACT = mybir.ActivationFunctionType
+MULT = mybir.AluOpType.mult
+
+P = 128
+PACK = 4
+PASS = 512
+HALF = 512
+GROUP = 128
+CHUNK = 256
+
+
+def tile_list_paged_gated_values_kernel(
+    tc, tab_words, tab_scales, offs, tab2_words, tab2_scales, offs2, wg, bg, wv_words, wv_scales, wo, bo, out
+):
+    nc = tc.nc
+    with ExitStack() as ctx:
+        keep = ctx.enter_context(tc.tile_pool(name="keep", bufs=1))
+        ring = ctx.enter_context(tc.tile_pool(name="ring", bufs=3))
+        psum = ctx.enter_context(tc.psum_pool(name="psum", bufs=1))
+
+        def held(shape, dtype, name):
+            return keep.tile(shape, dtype, name=name, align_bytes=64)
+
+        idx = keep.tile([P, S // 16], U16, name="idx")
+        idx2 = keep.tile([P, S // 16], U16, name="idx2")
+        v_words = [held([P, T], U32, f"v_words{a}") for a in range(2)]
+        v_scales = held([P, T], U8, "v_scales")
+        v2_words = keep.tile([P, T2], U32, name="v2_words", align_bytes=64)
+        v2_scales = held([P, T2], U8, "v2_scales")
+        wv_raw = held([P, 2 * H], U8, "wv_raw")
+        wv_raw_scales = held([P, H], U8, "wv_raw_scales")
+        wg_raw = [[held([P, PACK, PASS], F32, f"wg_raw{a}{b}") for b in range(2)] for a in range(2)]
+        wo_raw = [held([P, PACK, N], F32, f"wo_raw{b}") for b in range(2)]
+        bg_sb = held([P, 2, PACK], F32, "bg_sb")
+        bo_sb = held([P, N // P], F32, "bo_sb")
+
+        nc.vector.memset(v_scales[:].bitcast(I32), 0)
+        nc.vector.memset(wv_raw_scales[:].bitcast(I32), 0)
+        nc.gpsimd.memset(v2_scales[:].bitcast(I32), 0)
+
+        def load_words(dst, src):
+            nc.sync.dma_start(dst[:].bitcast(I32), src.rearrange("p t i -> p (t i)").bitcast(I32))
+
+        def load_scales(dst, src):
+            passes = src.shape[0]
+            for q in range(4):
+                nc.sync.dma_start(
+                    dst[32 * q : 32 * q + 4 * passes, :].bitcast(I32), src[:, 4 * q : 4 * q + 4, :].bitcast(I32)
+                )
+
+        def load_wg(a, b):
+            rows = wg[PASS * a : PASS * (a + 1), PASS * b : PASS * (b + 1)]
+            nc.sync.dma_start(wg_raw[a][b][:], rows.rearrange("(p j) c -> p j c", j=PACK))
+
+        nc.sync.dma_start(idx[:], offs)
+        load_wg(0, 0)
+        load_scales(v_scales, tab_scales)
+        load_words(v_words[0], tab_words[0])
+        nc.sync.dma_start(wv_raw[:].bitcast(I32), wv_words[0].bitcast(I32))
+        nc.sync.dma_start(idx2[:], offs2)
+        load_wg(1, 0)
+        load_scales(wv_raw_scales, wv_scales)
+        load_words(v_words[1], tab_words[1])
+        nc.sync.dma_start(bg_sb[:], bg.rearrange("(b p t) -> p b t", b=2, t=PACK))
+        load_scales(v2_scales, tab2_scales)
+        load_words(v2_words, tab2_words[0])
+        load_wg(0, 1)
+        load_wg(1, 1)
+        for b in range(2):
+            nc.sync.dma_start(wo_raw[b][:], wo[PASS * b : PASS * (b + 1), :].rearrange("(p j) n -> p j n", j=PACK))
+        nc.sync.dma_start(bo_sb[:], bo.rearrange("(p j) -> p j", j=PACK))
+
+        g_words = [held([P, S], U32, f"g_words{a}") for a in range(2)]
+        g_scales = held([P, S], U8, "g_scales")
+        a_words = held([P, S], U32, "a_words")
+        a_scales = held([P, S], U8, "a_scales")
+
+        def gather(dst, window, lst, pieces=1):
+            n = S // pieces
+            for i in range(pieces):
+                nc.vector.tensor_copy(
+                    dst[:, n * i : n * (i + 1)], window[:].indirect(lst[:, n // 16 * i : n // 16 * (i + 1)])
+                )
+
+        def deal_and_quantise(raw, name, on_scalar=P, tag=None):
+            wide = keep.tile([P, PACK * PASS], BF16, name=name + "_bf", tag=tag or name, align_bytes=64)
+            codes = held([P, PASS], U32, name + "_codes")
+            scales = held([P, PASS], U8, name + "_scales")
+            dst = wide[:].rearrange("p (u e m j) -> p u m j e", u=2, e=2, j=PACK)
+            src = raw[:].rearrange("p j (m u e) -> p u m j e", u=2, e=2)
+            if on_scalar > 0:
+                nc.scalar.copy(dst[:, :, :on_scalar], src[:, :, :on_scalar])
+            if on_scalar < P:
+                nc.vector.tensor_copy(dst[:, :, on_scalar:], src[:, :, on_scalar:])
+            nc.vector.quantize_mx(codes[:].bitcast(FP8X4), scales[:], wide[:])
+            return codes, scales
+
+        gather(g_scales, v_scales, idx)
+        gather(g_words[0], v_words[0], idx)
+        wv_codes = held([P, 2 * H], U8, "wv_codes")
+        wv_sc = held([P, H], U8, "wv_sc")
+        nc.vector.tensor_copy(
+            wv_codes[:].bitcast(U16).rearrange("p (b t m) -> p b t m", b=2, t=PACK),
+            wv_raw[:].bitcast(U16).rearrange("p (b m t) -> p b t m", b=2, t=PACK),
+        )
+        wgq = {(0, 0): deal_and_quantise(wg_raw[0][0], "wg00")}
+        nc.vector.tensor_copy(
+            wv_sc[:].rearrange("p (b t m) -> p b t m", b=2, t=PACK),
+            wv_raw_scales[:].rearrange("p (b m t) -> p b t m", b=2, t=PACK),
+        )
+        wgq[(1, 0)] = deal_and_quantise(wg_raw[1][0], "wg10")
+        gather(g_words[1], v_words[1], idx, pieces=2)
+        gather(a_scales, v2_scales, idx2)
+        gather(a_words, v2_words, idx2, pieces=2)
+
+        def gates(b, s):
+            sig = ring.tile([P, PACK, HALF], F32, name="sig", bufs=4)
+            for t in range(PACK):
+                bank = psum.tile([P, HALF], F32, name="g_bank", bufs=3)
+                for a in range(2):
+                    codes, scales = wgq[(a, b)]
+                    nc.tensor.matmul_mx(
+                        bank[:],
+                        lhsT=codes[:, P * t : P * (t + 1)].bitcast(FP8X4),
+                        lhsT_scale=scales[:, P * t : P * (t + 1)],
+                        rhs=g_words[a][:, HALF * s : HALF * (s + 1)].bitcast(FP8X4),
+                        rhs_scale=g_scales[4 * a :, HALF * s : HALF * (s + 1)],
+                        start=(a == 0),
+                        stop=(a == 1),
+                    )
+                nc.scalar.activation(sig[:, t, :], bank[:], ACT.Sigmoid, bias=bg_sb[:, b, t : t + 1])
+            return sig
+
+        h_codes = [held([P, S], U32, f"h_codes{b}") for b in range(2)]
+        h_scales = [held([P, S], U8, f"h_scales{b}") for b in range(2)]
+
+        def gated(b, first, width, sig, tag=None):
+            hb = keep.tile([P, width * PACK], BF16, name=f"hb{b}_{first}", tag=tag or f"hb{b}_{first}", align_bytes=64)
+            for u in range(width // GROUP):
+                tok = first + GROUP * u
+                lo = tok % HALF
+                bank = psum.tile([P, PACK, GROUP], F32, name="a_bank", bufs=2)
+                for t in range(PACK):
+                    col = PASS * b + P * t
+                    nc.tensor.matmul_mx(
+                        bank[:, t, :],
+                        lhsT=wv_codes[:, 2 * col : 2 * (col + P)].bitcast(FP4X4),
+                        lhsT_scale=wv_sc[:, col : col + P],
+                        rhs=a_words[:, tok : tok + GROUP].bitcast(FP8X4),
+                        rhs_scale=a_scales[:, tok : tok + GROUP],
+                        start=True,
+                        stop=True,
+                    )
+                nc.vector.tensor_tensor(
+                    hb[:, PACK * GROUP * u : PACK * GROUP * (u + 1)].rearrange("p (c e t) -> p c t e", e=2, t=PACK),
+                    bank[:].rearrange("p t (c e) -> p c t e", e=2),
+                    sig[:, :, lo : lo + GROUP].rearrange("p t (c e) -> p c t e", e=2),
+                    MULT,
+                )
+            nc.vector.quantize_mx(
+                h_codes[b][:, first : first + width].bitcast(FP8X4),
+                h_scales[b][:, first : first + width],
+                hb[:, : PACK * width],
+            )
+
+        sig0 = [gates(0, s) for s in range(2)]
+        wgq[(0, 1)] = deal_and_quantise(wg_raw[0][1], "wg01")
+        wgq[(1, 1)] = deal_and_quantise(wg_raw[1][1], "wg11", tag="late")
+        sig1 = [gates(1, s) for s in range(2)]
+        gated(0, 0, HALF, sig0[0])
+        gated(0, HALF, HALF, sig0[1], tag="late")
+        woq = [deal_and_quantise(wo_raw[0], "wo0"), deal_and_quantise(wo_raw[1], "wo1", on_scalar=64, tag="late")]
+
+        out_rows = out.rearrange("(p j) s -> p j s", j=PACK)
+        lo = 0
+        for width in (256, 256, 256, 128, 128):
+            gated(1, lo, width, sig1[lo // HALF])
+            res = keep.tile([P, PACK, width], F32, name=f"res{lo}")
+            for pair in range(2):
+                bank = psum.tile([P, 2, CHUNK], F32, name="y_bank", bufs=3)
+                for e in range(2):
+                    j = 2 * pair + e
+                    for b in range(2):
+                        nc.tensor.matmul_mx(
+                            bank[:, e, :width],
+                            lhsT=woq[b][0][:, P * j : P * (j + 1)].bitcast(FP8X4),
+                            lhsT_scale=woq[b][1][:, P * j : P * (j + 1)],
+                            rhs=h_codes[b][:, lo : lo + width].bitcast(FP8X4),
+                            rhs_scale=h_scales[b][:, lo : lo + width],
+                            start=(b == 0),
+                            stop=(b == 1),
+                        )
+                for e in range(2):
+                    j = 2 * pair + e
+                    if lo + width == S and pair == 1:
+                        nc.vector.tensor_scalar_add(res[:, j, :], bank[:, e, :width], bo_sb[:, j : j + 1])
+                    else:
+                        nc.scalar.activation(res[:, j, :], bank[:, e, :width], ACT.Identity, bias=bo_sb[:, j : j + 1])
+            nc.sync.dma_start(out_rows[:, :, lo : lo + width], res[:])
+            lo = lo + width

@@ -30,7 +30,7 @@ def tile_list_paged_gated_values_kernel(
     nc = tc.nc
     with ExitStack() as ctx:
         keep = ctx.enter_context(tc.tile_pool(name="keep", bufs=1))
-        ring = ctx.enter_context(tc.tile_pool(name="ring", bufs=3))
+        late = ctx.enter_context(tc.tile_pool(name="late", bufs=1))
         psum = ctx.enter_context(tc.psum_pool(name="psum", bufs=1))
 
         def held(shape, dtype, name):
@@ -40,12 +40,12 @@ def tile_list_paged_gated_values_kernel(
         idx2 = keep.tile([P, S // 16], U16, name="idx2")
         v_words = [held([P, T], U32, f"v_words{a}") for a in range(2)]
         v_scales = held([P, T], U8, "v_scales")
-        v2_words = keep.tile([P, T2], U32, name="v2_words", align_bytes=64)
-        v2_scales = held([P, T2], U8, "v2_scales")
+        v2_words = late.tile([P, T2], U32, name="v2_words", offset=0, align_bytes=64)
+        v2_scales = late.tile([P, T2], U8, name="v2_scales", offset=16384, align_bytes=64)
         wv_raw = held([P, 2 * H], U8, "wv_raw")
-        wv_raw_scales = held([P, H], U8, "wv_raw_scales")
+        wv_raw_scales = late.tile([P, H], U8, name="wv_raw_scales", offset=20480, align_bytes=64)
         wg_raw = [[held([P, PACK, PASS], F32, f"wg_raw{a}{b}") for b in range(2)] for a in range(2)]
-        wo_raw = [held([P, PACK, N], F32, f"wo_raw{b}") for b in range(2)]
+        wo_raw = [keep.tile([P, PACK, N], F32, name=f"wo_raw{b}", tag=f"wo_raw{b}") for b in range(2)]
         bg_sb = held([P, 2, PACK], F32, "bg_sb")
         bo_sb = held([P, N // P], F32, "bo_sb")
 
@@ -57,11 +57,8 @@ def tile_list_paged_gated_values_kernel(
             nc.sync.dma_start(dst[:].bitcast(I32), src.rearrange("p t i -> p (t i)").bitcast(I32))
 
         def load_scales(dst, src):
-            passes = src.shape[0]
-            for q in range(4):
-                nc.sync.dma_start(
-                    dst[32 * q : 32 * q + 4 * passes, :].bitcast(I32), src[:, 4 * q : 4 * q + 4, :].bitcast(I32)
-                )
+            for r in range(4):
+                nc.sync.dma_start(dst[r:P:32, :].bitcast(I32), src[0, r:16:4, :].bitcast(I32))
 
         def load_wg(a, b):
             rows = wg[PASS * a : PASS * (a + 1), PASS * b : PASS * (b + 1)]
@@ -69,7 +66,10 @@ def tile_list_paged_gated_values_kernel(
 
         nc.sync.dma_start(idx[:], offs)
         load_wg(0, 0)
-        load_scales(v_scales, tab_scales)
+        for q in range(4):
+            nc.sync.dma_start(
+                v_scales[32 * q : 32 * q + 8, :].bitcast(I32), tab_scales[:, 4 * q : 4 * q + 4, :].bitcast(I32)
+            )
         load_words(v_words[0], tab_words[0])
         nc.sync.dma_start(wv_raw[:].bitcast(I32), wv_words[0].bitcast(I32))
         nc.sync.dma_start(idx2[:], offs2)
@@ -87,7 +87,7 @@ def tile_list_paged_gated_values_kernel(
 
         g_words = [held([P, S], U32, f"g_words{a}") for a in range(2)]
         g_scales = held([P, S], U8, "g_scales")
-        a_words = held([P, S], U32, "a_words")
+        a_words = late.tile([P, S], U32, name="a_words", offset=17408, align_bytes=64)
         a_scales = held([P, S], U8, "a_scales")
 
         def gather(dst, window, lst, pieces=1):
@@ -97,8 +97,13 @@ def tile_list_paged_gated_values_kernel(
                     dst[:, n * i : n * (i + 1)], window[:].indirect(lst[:, n // 16 * i : n // 16 * (i + 1)])
                 )
 
-        def deal_and_quantise(raw, name, on_scalar=P, tag=None):
-            wide = keep.tile([P, PACK * PASS], BF16, name=name + "_bf", tag=tag or name, align_bytes=64)
+        def bf16_tile(width, name, slot):
+            if slot is None:
+                return held([P, width], BF16, name)
+            return late.tile([P, width], BF16, name=name, offset=4096 * slot, align_bytes=64)
+
+        def deal_and_quantise(raw, name, on_scalar=P, slot=None):
+            wide = bf16_tile(PACK * PASS, name + "_bf", slot)
             codes = held([P, PASS], U32, name + "_codes")
             scales = held([P, PASS], U8, name + "_scales")
             dst = wide[:].rearrange("p (u e m j) -> p u m j e", u=2, e=2, j=PACK)
@@ -123,15 +128,15 @@ def tile_list_paged_gated_values_kernel(
             wv_sc[:].rearrange("p (b t m) -> p b t m", b=2, t=PACK),
             wv_raw_scales[:].rearrange("p (b m t) -> p b t m", b=2, t=PACK),
         )
-        wgq[(1, 0)] = deal_and_quantise(wg_raw[1][0], "wg10")
+        wgq[(1, 0)] = deal_and_quantise(wg_raw[1][0], "wg10", on_scalar=64)
         gather(g_words[1], v_words[1], idx, pieces=2)
         gather(a_scales, v2_scales, idx2)
         gather(a_words, v2_words, idx2, pieces=2)
 
         def gates(b, s):
-            sig = ring.tile([P, PACK, HALF], F32, name="sig", bufs=4)
+            sig = keep.tile([P, PACK, HALF], F32, name=f"sig{b}{s}", tag="wo_raw0" if (b, s) == (1, 0) else f"sig{b}{s}")
             for t in range(PACK):
-                bank = psum.tile([P, HALF], F32, name="g_bank", bufs=3)
+                bank = psum.tile([P, HALF], F32, name="g_bank", tag="wide_bank", bufs=4)
                 for a in range(2):
                     codes, scales = wgq[(a, b)]
                     nc.tensor.matmul_mx(
@@ -149,12 +154,12 @@ def tile_list_paged_gated_values_kernel(
         h_codes = [held([P, S], U32, f"h_codes{b}") for b in range(2)]
         h_scales = [held([P, S], U8, f"h_scales{b}") for b in range(2)]
 
-        def gated(b, first, width, sig, tag=None):
-            hb = keep.tile([P, width * PACK], BF16, name=f"hb{b}_{first}", tag=tag or f"hb{b}_{first}", align_bytes=64)
+        def gated(b, first, width, sig, slot=None):
+            hb = bf16_tile(width * PACK, f"hb{b}_{first}", slot)
             for u in range(width // GROUP):
                 tok = first + GROUP * u
                 lo = tok % HALF
-                bank = psum.tile([P, PACK, GROUP], F32, name="a_bank", bufs=2)
+                bank = psum.tile([P, PACK, GROUP], F32, name="a_bank", bufs=4)
                 for t in range(PACK):
                     col = PASS * b + P * t
                     nc.tensor.matmul_mx(
@@ -179,12 +184,13 @@ def tile_list_paged_gated_values_kernel(
             )
 
         sig0 = [gates(0, s) for s in range(2)]
-        wgq[(0, 1)] = deal_and_quantise(wg_raw[0][1], "wg01")
-        wgq[(1, 1)] = deal_and_quantise(wg_raw[1][1], "wg11", tag="late")
+        wgq[(0, 1)] = deal_and_quantise(wg_raw[0][1], "wg01", slot=0)
+        wgq[(1, 1)] = deal_and_quantise(wg_raw[1][1], "wg11", on_scalar=96, slot=1)
+        woq = [deal_and_quantise(wo_raw[0], "wo0", slot=2)]
         sig1 = [gates(1, s) for s in range(2)]
         gated(0, 0, HALF, sig0[0])
-        gated(0, HALF, HALF, sig0[1], tag="late")
-        woq = [deal_and_quantise(wo_raw[0], "wo0"), deal_and_quantise(wo_raw[1], "wo1", on_scalar=64, tag="late")]
+        gated(0, HALF, HALF, sig0[1], slot=1)
+        woq.append(deal_and_quantise(wo_raw[1], "wo1", on_scalar=0, slot=1))
 
         out_rows = out.rearrange("(p j) s -> p j s", j=PACK)
         lo = 0
@@ -192,7 +198,7 @@ def tile_list_paged_gated_values_kernel(
             gated(1, lo, width, sig1[lo // HALF])
             res = keep.tile([P, PACK, width], F32, name=f"res{lo}")
             for pair in range(2):
-                bank = psum.tile([P, 2, CHUNK], F32, name="y_bank", bufs=3)
+                bank = psum.tile([P, 2, CHUNK], F32, name="y_bank", tag="wide_bank", bufs=4)
                 for e in range(2):
                     j = 2 * pair + e
                     for b in range(2):

@@ -185,12 +185,13 @@ def tile_list_paged_gated_values_kernel(
 
         sig0 = [gates(0, s) for s in range(2)]
         wgq[(0, 1)] = deal_and_quantise(wg_raw[0][1], "wg01", slot=0)
-        wgq[(1, 1)] = deal_and_quantise(wg_raw[1][1], "wg11", on_scalar=96, slot=1)
+        wgq[(1, 1)] = deal_and_quantise(wg_raw[1][1], "wg11", slot=1)
         woq = [deal_and_quantise(wo_raw[0], "wo0", slot=2)]
-        sig1 = [gates(1, s) for s in range(2)]
+        sig1 = [gates(1, 0)]
         gated(0, 0, HALF, sig0[0])
         gated(0, HALF, HALF, sig0[1], slot=1)
-        woq.append(deal_and_quantise(wo_raw[1], "wo1", on_scalar=0, slot=1))
+        woq.append(deal_and_quantise(wo_raw[1], "wo1", on_scalar=64, slot=1))
+        sig1.append(gates(1, 1))
 
         out_rows = out.rearrange("(p j) s -> p j s", j=PACK)
         lo = 0

@@ -15,6 +15,7 @@ FP8X4 = mybir.dt.float8_e4m3fn_x4
 FP4X4 = mybir.dt.float4_e2m1fn_x4
 ACT = mybir.ActivationFunctionType
 MULT = mybir.AluOpType.mult
+ADD = mybir.AluOpType.add
 
 P = 128
 PACK = 4
@@ -33,25 +34,35 @@ def tile_list_paged_gated_values_kernel(
         late = ctx.enter_context(tc.tile_pool(name="late", bufs=1))
         psum = ctx.enter_context(tc.psum_pool(name="psum", bufs=1))
 
-        def held(shape, dtype, name):
-            return keep.tile(shape, dtype, name=name, align_bytes=64)
+        def held(shape, dtype, name, offset=None):
+            if offset is None:
+                return keep.tile(shape, dtype, name=name, align_bytes=64)
+            return late.tile(shape, dtype, name=name, offset=offset, align_bytes=64)
 
         idx = keep.tile([P, S // 16], U16, name="idx")
         idx2 = keep.tile([P, S // 16], U16, name="idx2")
         v_words = [held([P, T], U32, f"v_words{a}") for a in range(2)]
         v_scales = held([P, T], U8, "v_scales")
-        v2_words = late.tile([P, T2], U32, name="v2_words", offset=0, align_bytes=64)
-        v2_scales = late.tile([P, T2], U8, name="v2_scales", offset=16384, align_bytes=64)
+        v2_words = held([P, T2], U32, "v2_words")
+        v2_scales = held([P, T2], U8, "v2_scales", offset=16384)
         wv_raw = held([P, 2 * H], U8, "wv_raw")
-        wv_raw_scales = late.tile([P, H], U8, name="wv_raw_scales", offset=20480, align_bytes=64)
+        wv_raw_scales = held([P, H], U8, "wv_raw_scales", offset=20480)
         wg_raw = [[held([P, PACK, PASS], F32, f"wg_raw{a}{b}") for b in range(2)] for a in range(2)]
-        wo_raw = [keep.tile([P, PACK, N], F32, name=f"wo_raw{b}", tag=f"wo_raw{b}") for b in range(2)]
+        wo_raw = [held([P, PACK, N], F32, f"wo_raw{b}") for b in range(2)]
         bg_sb = held([P, 2, PACK], F32, "bg_sb")
         bo_sb = held([P, N // P], F32, "bo_sb")
 
+        g_scales = held([P, 2, S], U8, "g_scales")
+        a_scales = held([P, S], U8, "a_scales")
+
         nc.vector.memset(v_scales[:].bitcast(I32), 0)
-        nc.vector.memset(wv_raw_scales[:].bitcast(I32), 0)
-        nc.gpsimd.memset(v2_scales[:].bitcast(I32), 0)
+        nc.vector.memset(v2_scales[:].bitcast(I32), 0)
+        nc.gpsimd.memset(wv_raw_scales[:].bitcast(I32), 0)
+        nc.gpsimd.memset(g_scales[:].bitcast(I32), 0)
+        nc.gpsimd.memset(a_scales[:].bitcast(I32), 0)
+        warm = held([P, 2], F32, "warm")
+        nc.vector.memset(warm[:, 0:1], 0.0)
+        nc.scalar.activation(warm[:, 1:2], warm[:, 0:1], ACT.Sigmoid)
 
         def load_words(dst, src):
             nc.sync.dma_start(dst[:].bitcast(I32), src.rearrange("p t i -> p (t i)").bitcast(I32))
@@ -64,31 +75,10 @@ def tile_list_paged_gated_values_kernel(
             rows = wg[PASS * a : PASS * (a + 1), PASS * b : PASS * (b + 1)]
             nc.sync.dma_start(wg_raw[a][b][:], rows.rearrange("(p j) c -> p j c", j=PACK))
 
-        nc.sync.dma_start(idx[:], offs)
-        load_wg(0, 0)
-        for q in range(4):
-            nc.sync.dma_start(
-                v_scales[32 * q : 32 * q + 8, :].bitcast(I32), tab_scales[:, 4 * q : 4 * q + 4, :].bitcast(I32)
-            )
-        load_words(v_words[0], tab_words[0])
-        nc.sync.dma_start(wv_raw[:].bitcast(I32), wv_words[0].bitcast(I32))
-        nc.sync.dma_start(idx2[:], offs2)
-        load_wg(1, 0)
-        load_scales(wv_raw_scales, wv_scales)
-        load_words(v_words[1], tab_words[1])
-        nc.sync.dma_start(bg_sb[:], bg.rearrange("(b p t) -> p b t", b=2, t=PACK))
-        load_scales(v2_scales, tab2_scales)
-        load_words(v2_words, tab2_words[0])
-        load_wg(0, 1)
-        load_wg(1, 1)
-        for b in range(2):
-            nc.sync.dma_start(wo_raw[b][:], wo[PASS * b : PASS * (b + 1), :].rearrange("(p j) n -> p j n", j=PACK))
-        nc.sync.dma_start(bo_sb[:], bo.rearrange("(p j) -> p j", j=PACK))
-
         g_words = [held([P, S], U32, f"g_words{a}") for a in range(2)]
-        g_scales = held([P, S], U8, "g_scales")
-        a_words = late.tile([P, S], U32, name="a_words", offset=17408, align_bytes=64)
-        a_scales = held([P, S], U8, "a_scales")
+        g_picked = held([P, S], U8, "g_picked")
+        a_words = held([P, S], U32, "a_words", offset=17408)
+        a_picked = held([P, S], U8, "a_picked")
 
         def gather(dst, window, lst, pieces=1):
             n = S // pieces
@@ -97,46 +87,94 @@ def tile_list_paged_gated_values_kernel(
                     dst[:, n * i : n * (i + 1)], window[:].indirect(lst[:, n // 16 * i : n // 16 * (i + 1)])
                 )
 
-        def bf16_tile(width, name, slot):
-            if slot is None:
-                return held([P, width], BF16, name)
-            return late.tile([P, width], BF16, name=name, offset=4096 * slot, align_bytes=64)
+        nc.sync.dma_start(idx[:], offs)
+        nc.sync.dma_start(wv_raw[:].bitcast(I32), wv_words[0].bitcast(I32))
+        for a in range(2):
+            nc.sync.dma_start(v_scales[4 * a : P : 8, :].bitcast(I32), tab_scales[a].bitcast(I32))
+        load_words(v_words[0], tab_words[0])
+        nc.sync.dma_start(idx2[:], offs2)
+        nc.sync.dma_start(v2_scales[0:P:8, :].bitcast(I32), tab2_scales[0].bitcast(I32))
+        load_wg(0, 0)
+        load_scales(wv_raw_scales, wv_scales)
+        load_wg(1, 0)
+        gather(g_picked, v_scales, idx)
+        for q in range(4):
+            nc.sync.dma_start(
+                g_scales[32 * q + 4 : 32 * q + 8].rearrange("p a s -> p (a s)").bitcast(I32),
+                g_picked[32 * q : 32 * (q + 1) : 4, :].bitcast(I32),
+            )
+        load_words(v_words[1], tab_words[1])
+        nc.sync.dma_start(bg_sb[:], bg.rearrange("(b p t) -> p b t", b=2, t=PACK))
+        load_words(v2_words, tab2_words[0])
+        gather(a_picked, v2_scales, idx2)
+        for q in range(4):
+            nc.sync.dma_start(
+                a_scales[32 * q : 32 * q + 4, :].bitcast(I32), a_picked[32 * q : 32 * (q + 1) : 8, :].bitcast(I32)
+            )
+        load_wg(0, 1)
+        load_wg(1, 1)
+        for b in range(2):
+            nc.sync.dma_start(wo_raw[b][:], wo[PASS * b : PASS * (b + 1), :].rearrange("(p j) n -> p j n", j=PACK))
+        with nc.allow_non_contiguous_dma(reason="one bias value a partition"):
+            nc.sync.dma_start(bo_sb[:], bo.rearrange("(j p) -> p j", p=P))
 
-        def deal_and_quantise(raw, name, on_scalar=P, slot=None):
-            wide = bf16_tile(PACK * PASS, name + "_bf", slot)
-            codes = held([P, PASS], U32, name + "_codes")
-            scales = held([P, PASS], U8, name + "_scales")
-            dst = wide[:].rearrange("p (u e m j) -> p u m j e", u=2, e=2, j=PACK)
-            src = raw[:].rearrange("p j (m u e) -> p u m j e", u=2, e=2)
-            if on_scalar > 0:
-                nc.scalar.copy(dst[:, :, :on_scalar], src[:, :, :on_scalar])
-            if on_scalar < P:
-                nc.vector.tensor_copy(dst[:, :, on_scalar:], src[:, :, on_scalar:])
+        def round_wg(a, b, offset=None):
+            wide = held([P, PACK * PASS], BF16, f"wg_bf{a}{b}", offset)
+            nc.scalar.copy(
+                wide[:].rearrange("p (u e m j) -> p u m j e", u=2, e=2, j=PACK),
+                wg_raw[a][b][:].rearrange("p j (m u e) -> p u m j e", u=2, e=2),
+            )
+            return wide
+
+        def quantise_wg(a, b, wide):
+            codes = held([P, PASS], U32, f"wg_codes{a}{b}")
+            scales = held([P, PASS], U8, f"wg_scales{a}{b}")
             nc.vector.quantize_mx(codes[:].bitcast(FP8X4), scales[:], wide[:])
             return codes, scales
 
-        gather(g_scales, v_scales, idx)
+        def round_wo(b, first, width, engine, offset=None):
+            wide = held([P, PACK * width], BF16, f"wo_bf{b}_{first}", offset)
+            dst = wide[:].rearrange("p (m e j) -> p m j e", e=2, j=PACK)
+            src = wo_raw[b][:, :, first : first + width].rearrange("p j (m e) -> p m j e", e=2)
+            if engine == "scalar":
+                nc.scalar.copy(dst, src)
+            elif engine == "vector":
+                nc.vector.tensor_copy(dst, src)
+            else:
+                nc.gpsimd.tensor_scalar(dst, src, 1.0, 0.0, MULT, ADD)
+            return wide
+
+        wo_codes = [held([P, N], U32, f"wo_codes{b}") for b in range(2)]
+        wo_scales = [held([P, N], U8, f"wo_scales{b}") for b in range(2)]
+
+        def quantise_wo(b, first, width, wide):
+            cols = slice(first, first + width)
+            nc.vector.quantize_mx(wo_codes[b][:, cols].bitcast(FP8X4), wo_scales[b][:, cols], wide[:])
+
         gather(g_words[0], v_words[0], idx)
+        wgq = {}
+        for a in range(2):
+            wgq[(a, 0)] = quantise_wg(a, 0, round_wg(a, 0))
+        gather(g_words[1], v_words[1], idx, pieces=2)
         wv_codes = held([P, 2 * H], U8, "wv_codes")
         wv_sc = held([P, H], U8, "wv_sc")
         nc.vector.tensor_copy(
             wv_codes[:].bitcast(U16).rearrange("p (b t m) -> p b t m", b=2, t=PACK),
             wv_raw[:].bitcast(U16).rearrange("p (b m t) -> p b t m", b=2, t=PACK),
         )
-        wgq = {(0, 0): deal_and_quantise(wg_raw[0][0], "wg00")}
         nc.vector.tensor_copy(
             wv_sc[:].rearrange("p (b t m) -> p b t m", b=2, t=PACK),
             wv_raw_scales[:].rearrange("p (b m t) -> p b t m", b=2, t=PACK),
         )
-        wgq[(1, 0)] = deal_and_quantise(wg_raw[1][0], "wg10", on_scalar=64)
-        gather(g_words[1], v_words[1], idx, pieces=2)
-        gather(a_scales, v2_scales, idx2)
         gather(a_words, v2_words, idx2, pieces=2)
 
-        def gates(b, s):
-            sig = keep.tile([P, PACK, HALF], F32, name=f"sig{b}{s}", tag="wo_raw0" if (b, s) == (1, 0) else f"sig{b}{s}")
+        sig = {}
+
+        def gates(b, s, width):
+            banks = []
             for t in range(PACK):
                 bank = psum.tile([P, HALF], F32, name="g_bank", tag="wide_bank", bufs=4)
+                banks.append(bank)
                 for a in range(2):
                     codes, scales = wgq[(a, b)]
                     nc.tensor.matmul_mx(
@@ -144,79 +182,132 @@ def tile_list_paged_gated_values_kernel(
                         lhsT=codes[:, P * t : P * (t + 1)].bitcast(FP8X4),
                         lhsT_scale=scales[:, P * t : P * (t + 1)],
                         rhs=g_words[a][:, HALF * s : HALF * (s + 1)].bitcast(FP8X4),
-                        rhs_scale=g_scales[4 * a :, HALF * s : HALF * (s + 1)],
+                        rhs_scale=g_scales[4:, a, HALF * s : HALF * (s + 1)],
                         start=(a == 0),
                         stop=(a == 1),
                     )
-                nc.scalar.activation(sig[:, t, :], bank[:], ACT.Sigmoid, bias=bg_sb[:, b, t : t + 1])
-            return sig
+            for lo in range(0, HALF, width):
+                gate = held([P, PACK, width], F32, f"sig{b}{s}_{lo}")
+                for u in range(width // GROUP):
+                    sig[(b, HALF * s + lo + GROUP * u)] = gate[:, :, GROUP * u : GROUP * (u + 1)]
+                for t in range(PACK):
+                    nc.scalar.activation(
+                        gate[:, t, :], banks[t][:, lo : lo + width], ACT.Sigmoid, bias=bg_sb[:, b, t : t + 1]
+                    )
 
-        h_codes = [held([P, S], U32, f"h_codes{b}") for b in range(2)]
+        h0_codes = held([P, S], U32, "h0_codes")
         h_scales = [held([P, S], U8, f"h_scales{b}") for b in range(2)]
 
-        def gated(b, first, width, sig, slot=None):
-            hb = bf16_tile(width * PACK, f"hb{b}_{first}", slot)
+        groups = [(b, tok) for b in range(2) for tok in range(0, S, GROUP)]
+        values = {}
+
+        def project_values(g):
+            b, tok = groups[g]
+            bank = psum.tile([P, PACK, GROUP], F32, name="a_bank", tag="a_bank", bufs=4)
+            for t in range(PACK):
+                col = PASS * b + P * t
+                nc.tensor.matmul_mx(
+                    bank[:, t, :],
+                    lhsT=wv_codes[:, 2 * col : 2 * (col + P)].bitcast(FP4X4),
+                    lhsT_scale=wv_sc[:, col : col + P],
+                    rhs=a_words[:, tok : tok + GROUP].bitcast(FP8X4),
+                    rhs_scale=a_scales[:, tok : tok + GROUP],
+                    start=True,
+                    stop=True,
+                )
+            values[groups[g]] = bank
+
+        def gate_values(b, first, width, offset=None):
+            hb = held([P, width * PACK], BF16, f"hb{b}_{first}", offset)
             for u in range(width // GROUP):
                 tok = first + GROUP * u
-                lo = tok % HALF
-                bank = psum.tile([P, PACK, GROUP], F32, name="a_bank", bufs=4)
-                for t in range(PACK):
-                    col = PASS * b + P * t
-                    nc.tensor.matmul_mx(
-                        bank[:, t, :],
-                        lhsT=wv_codes[:, 2 * col : 2 * (col + P)].bitcast(FP4X4),
-                        lhsT_scale=wv_sc[:, col : col + P],
-                        rhs=a_words[:, tok : tok + GROUP].bitcast(FP8X4),
-                        rhs_scale=a_scales[:, tok : tok + GROUP],
-                        start=True,
-                        stop=True,
-                    )
                 nc.vector.tensor_tensor(
                     hb[:, PACK * GROUP * u : PACK * GROUP * (u + 1)].rearrange("p (c e t) -> p c t e", e=2, t=PACK),
-                    bank[:].rearrange("p t (c e) -> p c t e", e=2),
-                    sig[:, :, lo : lo + GROUP].rearrange("p t (c e) -> p c t e", e=2),
+                    values[(b, tok)][:].rearrange("p t (c e) -> p c t e", e=2),
+                    sig[(b, tok)].rearrange("p t (c e) -> p c t e", e=2),
                     MULT,
                 )
-            nc.vector.quantize_mx(
-                h_codes[b][:, first : first + width].bitcast(FP8X4),
-                h_scales[b][:, first : first + width],
-                hb[:, : PACK * width],
-            )
+                ahead = groups.index((b, tok)) + 4
+                if ahead < len(groups):
+                    project_values(ahead)
+            return hb
 
-        sig0 = [gates(0, s) for s in range(2)]
-        wgq[(0, 1)] = deal_and_quantise(wg_raw[0][1], "wg01", slot=0)
-        wgq[(1, 1)] = deal_and_quantise(wg_raw[1][1], "wg11", slot=1)
-        woq = [deal_and_quantise(wo_raw[0], "wo0", slot=2)]
-        sig1 = [gates(1, 0)]
-        gated(0, 0, HALF, sig0[0])
-        gated(0, HALF, HALF, sig0[1], slot=1)
-        woq.append(deal_and_quantise(wo_raw[1], "wo1", on_scalar=64, slot=1))
-        sig1.append(gates(1, 1))
+        def quantise_h(b, first, width, hb, codes):
+            nc.vector.quantize_mx(codes.bitcast(FP8X4), h_scales[b][:, first : first + width], hb[:])
 
-        out_rows = out.rearrange("(p j) s -> p j s", j=PACK)
-        lo = 0
-        for width in (256, 256, 256, 128, 128):
-            gated(1, lo, width, sig1[lo // HALF])
-            res = keep.tile([P, PACK, width], F32, name=f"res{lo}")
-            for pair in range(2):
-                bank = psum.tile([P, 2, CHUNK], F32, name="y_bank", tag="wide_bank", bufs=4)
+        gates(0, 0, HALF)
+        gates(0, 1, HALF)
+        for g in range(4):
+            project_values(g)
+        wg01 = round_wg(0, 1)
+        wg11 = round_wg(1, 1, offset=8192)
+        wo0a = round_wo(0, 0, CHUNK, "scalar")
+        hb_a = gate_values(0, 0, HALF)
+        wgq[(0, 1)] = quantise_wg(0, 1, wg01)
+        hb_b = gate_values(0, HALF, CHUNK)
+        quantise_h(0, 0, HALF, hb_a, h0_codes[:, :HALF])
+        wgq[(1, 1)] = quantise_wg(1, 1, wg11)
+        gates(1, 0, CHUNK)
+        wo0b = round_wo(0, CHUNK, CHUNK, "gpsimd", offset=10240)
+        hb_c = gate_values(0, HALF + CHUNK, CHUNK, offset=8192)
+        quantise_h(0, HALF, CHUNK, hb_b, h0_codes[:, HALF : HALF + CHUNK])
+        quantise_wo(0, 0, CHUNK, wo0a)
+        quantise_h(0, HALF + CHUNK, CHUNK, hb_c, h0_codes[:, HALF + CHUNK :])
+        quantise_wo(0, CHUNK, CHUNK, wo0b)
+        gates(1, 1, CHUNK)
+        wo1 = round_wo(1, 0, N, "gpsimd", offset=7168)
+
+        out_rows = out.rearrange("(j p) s -> p j s", p=P)
+
+        def project(lo, width, codes):
+            tag = "wide_bank" if width == CHUNK else "a_bank"
+            banks = [psum.tile([P, 2, CHUNK], F32, name="y_bank", tag=tag, bufs=4) for pair in range(2)]
+            for b in range(2):
+                for j in range(PACK):
+                    nc.tensor.matmul_mx(
+                        banks[j // 2][:, j % 2, :width],
+                        lhsT=wo_codes[b][:, P * j : P * (j + 1)].bitcast(FP8X4),
+                        lhsT_scale=wo_scales[b][:, P * j : P * (j + 1)],
+                        rhs=(h0_codes[:, lo : lo + width] if b == 0 else codes).bitcast(FP8X4),
+                        rhs_scale=h_scales[b][:, lo : lo + width],
+                        start=(b == 0 and j % 2 == 0),
+                        stop=(b == 1 and j % 2 == 1),
+                    )
+            return banks
+
+        def store(lo, width, pair, bank, on_vector=False, offset=None):
+            res = held([P, 2, width], F32, f"res{lo}_{pair}", offset)
+            if on_vector:
+                bias = bo_sb[:, 2 * pair : 2 * pair + 2].unsqueeze(2).to_broadcast([P, 2, width])
+                nc.vector.tensor_tensor(res[:], bank[:, :, :width], bias, ADD)
+            else:
                 for e in range(2):
                     j = 2 * pair + e
-                    for b in range(2):
-                        nc.tensor.matmul_mx(
-                            bank[:, e, :width],
-                            lhsT=woq[b][0][:, P * j : P * (j + 1)].bitcast(FP8X4),
-                            lhsT_scale=woq[b][1][:, P * j : P * (j + 1)],
-                            rhs=h_codes[b][:, lo : lo + width].bitcast(FP8X4),
-                            rhs_scale=h_scales[b][:, lo : lo + width],
-                            start=(b == 0),
-                            stop=(b == 1),
-                        )
-                for e in range(2):
-                    j = 2 * pair + e
-                    if lo + width == S and pair == 1:
-                        nc.vector.tensor_scalar_add(res[:, j, :], bank[:, e, :width], bo_sb[:, j : j + 1])
-                    else:
-                        nc.scalar.activation(res[:, j, :], bank[:, e, :width], ACT.Identity, bias=bo_sb[:, j : j + 1])
-            nc.sync.dma_start(out_rows[:, :, lo : lo + width], res[:])
-            lo = lo + width
+                    nc.scalar.activation(res[:, e, :], bank[:, e, :width], ACT.Identity, bias=bo_sb[:, j : j + 1])
+            nc.sync.dma_start(out_rows[:, 2 * pair : 2 * pair + 2, lo : lo + width], res[:])
+
+        hb_0 = gate_values(1, 0, CHUNK, offset=11264)
+        hb_1 = gate_values(1, CHUNK, CHUNK)
+        quantise_wo(1, 0, N, wo1)
+        codes = [held([P, CHUNK], U32, f"h1_codes{c}", offset=6208 + 1024 * c) for c in range(2)]
+        codes.extend(held([P, CHUNK], U32, f"h1_codes{c}") for c in range(2, 4))
+        quantise_h(1, 0, CHUNK, hb_0, codes[0][:])
+        for pair, bank in enumerate(project(0, CHUNK, codes[0][:])):
+            store(0, CHUNK, pair, bank)
+        hb_2 = gate_values(1, 2 * CHUNK, CHUNK, offset=8256)
+        quantise_h(1, CHUNK, CHUNK, hb_1, codes[1][:])
+        for pair, bank in enumerate(project(CHUNK, CHUNK, codes[1][:])):
+            store(CHUNK, CHUNK, pair, bank)
+        hb_3 = gate_values(1, 3 * CHUNK, GROUP, offset=10304)
+        quantise_h(1, 2 * CHUNK, CHUNK, hb_2, codes[2][:])
+        banks_2 = project(2 * CHUNK, CHUNK, codes[2][:])
+        store(2 * CHUNK, CHUNK, 0, banks_2[0])
+        hb_4 = gate_values(1, 3 * CHUNK + GROUP, GROUP, offset=11328)
+        quantise_h(1, 3 * CHUNK, GROUP, hb_3, codes[3][:, :GROUP])
+        banks_3 = project(3 * CHUNK, GROUP, codes[3][:, :GROUP])
+        quantise_h(1, 3 * CHUNK + GROUP, GROUP, hb_4, codes[3][:, GROUP:])
+        banks_4 = project(3 * CHUNK + GROUP, GROUP, codes[3][:, GROUP:])
+        store(2 * CHUNK, CHUNK, 1, banks_2[1], on_vector=True, offset=12288)
+        for lo, banks in ((3 * CHUNK, banks_3), (3 * CHUNK + GROUP, banks_4)):
+            store(lo, GROUP, 0, banks[0])
+            store(lo, GROUP, 1, banks[1], on_vector=True)

@@ -118,12 +118,15 @@ def tile_list_paged_gated_values_kernel(
         with nc.allow_non_contiguous_dma(reason="one bias value a partition"):
             nc.sync.dma_start(bo_sb[:], bo.rearrange("(j p) -> p j", p=P))
 
-        def round_wg(a, b, offset=None):
+        def round_wg(a, b, offset=None, second=None):
             wide = held([P, PACK * PASS], BF16, f"wg_bf{a}{b}", offset)
-            nc.scalar.copy(
-                wide[:].rearrange("p (u e m j) -> p u m j e", u=2, e=2, j=PACK),
-                wg_raw[a][b][:].rearrange("p j (m u e) -> p u m j e", u=2, e=2),
-            )
+            dst = wide[:].rearrange("p (u e m j) -> p u m j e", u=2, e=2, j=PACK)
+            src = wg_raw[a][b][:].rearrange("p j (m u e) -> p u m j e", u=2, e=2)
+            if second is None:
+                nc.scalar.copy(dst, src)
+            else:
+                nc.scalar.copy(dst[:, :, :64], src[:, :, :64])
+                second(dst[:, :, 64:], src[:, :, 64:])
             return wide
 
         def quantise_wg(a, b, wide):
@@ -132,9 +135,9 @@ def tile_list_paged_gated_values_kernel(
             nc.vector.quantize_mx(codes[:].bitcast(FP8X4), scales[:], wide[:])
             return codes, scales
 
-        def round_wo(b, first, width, engine, offset=None):
-            wide = held([P, PACK * width], BF16, f"wo_bf{b}_{first}", offset)
-            dst = wide[:].rearrange("p (m e j) -> p m j e", e=2, j=PACK)
+        def round_wo(b, first, width, engine, offset=None, room=1):
+            wide = held([P, room * PACK * width], BF16, f"wo_bf{b}_{first}", offset)[:, : PACK * width]
+            dst = wide.rearrange("p (m e j) -> p m j e", e=2, j=PACK)
             src = wo_raw[b][:, :, first : first + width].rearrange("p j (m e) -> p m j e", e=2)
             if engine == "scalar":
                 nc.scalar.copy(dst, src)
@@ -149,12 +152,12 @@ def tile_list_paged_gated_values_kernel(
 
         def quantise_wo(b, first, width, wide):
             cols = slice(first, first + width)
-            nc.vector.quantize_mx(wo_codes[b][:, cols].bitcast(FP8X4), wo_scales[b][:, cols], wide[:])
+            nc.vector.quantize_mx(wo_codes[b][:, cols].bitcast(FP8X4), wo_scales[b][:, cols], wide)
 
         gather(g_words[0], v_words[0], idx)
         wgq = {}
-        for a in range(2):
-            wgq[(a, 0)] = quantise_wg(a, 0, round_wg(a, 0))
+        wgq[(0, 0)] = quantise_wg(0, 0, round_wg(0, 0))
+        wgq[(1, 0)] = quantise_wg(1, 0, round_wg(1, 0, second=nc.vector.tensor_copy))
         gather(g_words[1], v_words[1], idx, pieces=2)
         wv_codes = held([P, 2 * H], U8, "wv_codes")
         wv_sc = held([P, H], U8, "wv_sc")
@@ -173,7 +176,7 @@ def tile_list_paged_gated_values_kernel(
         def gates(b, s, width):
             banks = []
             for t in range(PACK):
-                bank = psum.tile([P, HALF], F32, name="g_bank", tag="wide_bank", bufs=4)
+                bank = psum.tile([P, HALF], F32, name="g_bank", tag=f"wide{t}")
                 banks.append(bank)
                 for a in range(2):
                     codes, scales = wgq[(a, b)]
@@ -187,12 +190,15 @@ def tile_list_paged_gated_values_kernel(
                         stop=(a == 1),
                     )
             for lo in range(0, HALF, width):
-                gate = held([P, PACK, width], F32, f"sig{b}{s}_{lo}")
+                gate = held([P, width // 4, PACK, 4], F32, f"sig{b}{s}_{lo}")
                 for u in range(width // GROUP):
-                    sig[(b, HALF * s + lo + GROUP * u)] = gate[:, :, GROUP * u : GROUP * (u + 1)]
+                    sig[(b, HALF * s + lo + GROUP * u)] = gate[:, GROUP // 4 * u : GROUP // 4 * (u + 1)]
                 for t in range(PACK):
                     nc.scalar.activation(
-                        gate[:, t, :], banks[t][:, lo : lo + width], ACT.Sigmoid, bias=bg_sb[:, b, t : t + 1]
+                        gate[:, :, t, :],
+                        banks[t][:, lo : lo + width].rearrange("p (c e) -> p c e", e=4),
+                        ACT.Sigmoid,
+                        bias=bg_sb[:, b, t : t + 1],
                     )
 
         h0_codes = held([P, S], U32, "h0_codes")
@@ -203,7 +209,7 @@ def tile_list_paged_gated_values_kernel(
 
         def project_values(g):
             b, tok = groups[g]
-            bank = psum.tile([P, PACK, GROUP], F32, name="a_bank", tag="a_bank", bufs=4)
+            bank = psum.tile([P, PACK, GROUP], F32, name="a_bank", tag=f"value{g % 4}")
             for t in range(PACK):
                 col = PASS * b + P * t
                 nc.tensor.matmul_mx(
@@ -222,9 +228,9 @@ def tile_list_paged_gated_values_kernel(
             for u in range(width // GROUP):
                 tok = first + GROUP * u
                 nc.vector.tensor_tensor(
-                    hb[:, PACK * GROUP * u : PACK * GROUP * (u + 1)].rearrange("p (c e t) -> p c t e", e=2, t=PACK),
-                    values[(b, tok)][:].rearrange("p t (c e) -> p c t e", e=2),
-                    sig[(b, tok)].rearrange("p t (c e) -> p c t e", e=2),
+                    hb[:, PACK * GROUP * u : PACK * GROUP * (u + 1)].rearrange("p (c e t) -> p c t e", e=4, t=PACK),
+                    values[(b, tok)][:].rearrange("p t (c e) -> p c t e", e=4),
+                    sig[(b, tok)],
                     MULT,
                 )
                 ahead = groups.index((b, tok)) + 4
@@ -248,31 +254,37 @@ def tile_list_paged_gated_values_kernel(
         quantise_h(0, 0, HALF, hb_a, h0_codes[:, :HALF])
         wgq[(1, 1)] = quantise_wg(1, 1, wg11)
         gates(1, 0, CHUNK)
-        wo0b = round_wo(0, CHUNK, CHUNK, "gpsimd", offset=10240)
+        wo0b = round_wo(0, CHUNK, CHUNK, "gpsimd", offset=10240, room=2)
         hb_c = gate_values(0, HALF + CHUNK, CHUNK, offset=8192)
         quantise_h(0, HALF, CHUNK, hb_b, h0_codes[:, HALF : HALF + CHUNK])
         quantise_wo(0, 0, CHUNK, wo0a)
         quantise_h(0, HALF + CHUNK, CHUNK, hb_c, h0_codes[:, HALF + CHUNK :])
         quantise_wo(0, CHUNK, CHUNK, wo0b)
-        gates(1, 1, CHUNK)
-        wo1 = round_wo(1, 0, N, "gpsimd", offset=7168)
+        gates(1, 1, HALF)
+        wo1b = round_wo(1, CHUNK, CHUNK, "gpsimd", offset=8256)
+        wo1a = round_wo(1, 0, CHUNK, "gpsimd", offset=10304)
 
         out_rows = out.rearrange("(j p) s -> p j s", p=P)
 
-        def project(lo, width, codes):
-            tag = "wide_bank" if width == CHUNK else "a_bank"
-            banks = [psum.tile([P, 2, CHUNK], F32, name="y_bank", tag=tag, bufs=4) for pair in range(2)]
-            for b in range(2):
-                for j in range(PACK):
-                    nc.tensor.matmul_mx(
-                        banks[j // 2][:, j % 2, :width],
-                        lhsT=wo_codes[b][:, P * j : P * (j + 1)].bitcast(FP8X4),
-                        lhsT_scale=wo_scales[b][:, P * j : P * (j + 1)],
-                        rhs=(h0_codes[:, lo : lo + width] if b == 0 else codes).bitcast(FP8X4),
-                        rhs_scale=h_scales[b][:, lo : lo + width],
-                        start=(b == 0 and j % 2 == 0),
-                        stop=(b == 1 and j % 2 == 1),
-                    )
+        def project(lo, width, codes, early=True):
+            kind = "wide" if width == CHUNK else "value"
+            first = 2 * (lo // width % 2)
+            banks = [psum.tile([P, 2, CHUNK], F32, name="y_bank", tag=f"{kind}{first + i}") for i in range(2)]
+            if early:
+                order = [(b, j) for b in range(2) for j in range(PACK)]
+            else:
+                order = [(b, j) for j in range(PACK) for b in (1, 0)]
+            for b, j in order:
+                mates = [o for o in order if o[1] // 2 == j // 2]
+                nc.tensor.matmul_mx(
+                    banks[j // 2][:, j % 2, :width],
+                    lhsT=wo_codes[b][:, P * j : P * (j + 1)].bitcast(FP8X4),
+                    lhsT_scale=wo_scales[b][:, P * j : P * (j + 1)],
+                    rhs=(h0_codes[:, lo : lo + width] if b == 0 else codes).bitcast(FP8X4),
+                    rhs_scale=h_scales[b][:, lo : lo + width],
+                    start=(b, j) == mates[0],
+                    stop=(b, j) == mates[-1],
+                )
             return banks
 
         def store(lo, width, pair, bank, on_vector=False, offset=None):
@@ -286,28 +298,29 @@ def tile_list_paged_gated_values_kernel(
                     nc.scalar.activation(res[:, e, :], bank[:, e, :width], ACT.Identity, bias=bo_sb[:, j : j + 1])
             nc.sync.dma_start(out_rows[:, 2 * pair : 2 * pair + 2, lo : lo + width], res[:])
 
-        hb_0 = gate_values(1, 0, CHUNK, offset=11264)
+        hb_0 = gate_values(1, 0, CHUNK, offset=12352)
         hb_1 = gate_values(1, CHUNK, CHUNK)
-        quantise_wo(1, 0, N, wo1)
-        codes = [held([P, CHUNK], U32, f"h1_codes{c}", offset=6208 + 1024 * c) for c in range(2)]
+        quantise_wo(1, 0, CHUNK, wo1a)
+        codes = [held([P, CHUNK], U32, f"h1_codes{c}", offset=10304 + 1024 * c) for c in range(2)]
         codes.extend(held([P, CHUNK], U32, f"h1_codes{c}") for c in range(2, 4))
         quantise_h(1, 0, CHUNK, hb_0, codes[0][:])
+        quantise_wo(1, CHUNK, CHUNK, wo1b)
         for pair, bank in enumerate(project(0, CHUNK, codes[0][:])):
             store(0, CHUNK, pair, bank)
-        hb_2 = gate_values(1, 2 * CHUNK, CHUNK, offset=8256)
         quantise_h(1, CHUNK, CHUNK, hb_1, codes[1][:])
-        for pair, bank in enumerate(project(CHUNK, CHUNK, codes[1][:])):
+        for pair, bank in enumerate(project(CHUNK, CHUNK, codes[1][:], early=False)):
             store(CHUNK, CHUNK, pair, bank)
-        hb_3 = gate_values(1, 3 * CHUNK, GROUP, offset=10304)
+        hb_2 = gate_values(1, 2 * CHUNK, CHUNK, offset=8256)
+        hb_3 = gate_values(1, 3 * CHUNK, GROUP, offset=12352)
         quantise_h(1, 2 * CHUNK, CHUNK, hb_2, codes[2][:])
         banks_2 = project(2 * CHUNK, CHUNK, codes[2][:])
         store(2 * CHUNK, CHUNK, 0, banks_2[0])
-        hb_4 = gate_values(1, 3 * CHUNK + GROUP, GROUP, offset=11328)
+        hb_4 = gate_values(1, 3 * CHUNK + GROUP, GROUP, offset=13376)
         quantise_h(1, 3 * CHUNK, GROUP, hb_3, codes[3][:, :GROUP])
-        banks_3 = project(3 * CHUNK, GROUP, codes[3][:, :GROUP])
+        banks_3 = project(3 * CHUNK, GROUP, codes[3][:, :GROUP], early=False)
         quantise_h(1, 3 * CHUNK + GROUP, GROUP, hb_4, codes[3][:, GROUP:])
         banks_4 = project(3 * CHUNK + GROUP, GROUP, codes[3][:, GROUP:])
-        store(2 * CHUNK, CHUNK, 1, banks_2[1], on_vector=True, offset=12288)
+        store(2 * CHUNK, CHUNK, 1, banks_2[1], on_vector=True, offset=14336)
         for lo, banks in ((3 * CHUNK, banks_3), (3 * CHUNK + GROUP, banks_4)):
             store(lo, GROUP, 0, banks[0])
             store(lo, GROUP, 1, banks[1], on_vector=True)

@@ -60,9 +60,6 @@ def tile_list_paged_gated_values_kernel(
         nc.gpsimd.memset(wv_raw_scales[:].bitcast(I32), 0)
         nc.gpsimd.memset(g_scales[:].bitcast(I32), 0)
         nc.gpsimd.memset(a_scales[:].bitcast(I32), 0)
-        warm = held([P, 2], F32, "warm")
-        nc.vector.memset(warm[:, 0:1], 0.0)
-        nc.scalar.activation(warm[:, 1:2], warm[:, 0:1], ACT.Sigmoid)
 
         def load_words(dst, src):
             nc.sync.dma_start(dst[:].bitcast(I32), src.rearrange("p t i -> p (t i)").bitcast(I32))
@@ -147,12 +144,12 @@ def tile_list_paged_gated_values_kernel(
                 nc.gpsimd.tensor_scalar(dst, src, 1.0, 0.0, MULT, ADD)
             return wide
 
-        wo_codes = [held([P, N], U32, f"wo_codes{b}") for b in range(2)]
-        wo_scales = [held([P, N], U8, f"wo_scales{b}") for b in range(2)]
+        wo_codes = {(b, h): held([P, CHUNK], U32, f"wo_codes{b}{h}", 0 if (b, h) == (1, 0) else None) for b in range(2) for h in range(2)}
+        wo_scales = {(b, h): held([P, CHUNK], U8, f"wo_scales{b}{h}") for b in range(2) for h in range(2)}
 
         def quantise_wo(b, first, width, wide):
-            cols = slice(first, first + width)
-            nc.vector.quantize_mx(wo_codes[b][:, cols].bitcast(FP8X4), wo_scales[b][:, cols], wide)
+            key = (b, first // CHUNK)
+            nc.vector.quantize_mx(wo_codes[key][:].bitcast(FP8X4), wo_scales[key][:], wide)
 
         gather(g_words[0], v_words[0], idx)
         wgq = {}
@@ -173,34 +170,36 @@ def tile_list_paged_gated_values_kernel(
 
         sig = {}
 
-        def gates(b, s, width):
-            banks = []
-            for t in range(PACK):
-                bank = psum.tile([P, HALF], F32, name="g_bank", tag=f"wide{t}")
-                banks.append(bank)
-                for a in range(2):
-                    codes, scales = wgq[(a, b)]
-                    nc.tensor.matmul_mx(
-                        bank[:],
-                        lhsT=codes[:, P * t : P * (t + 1)].bitcast(FP8X4),
-                        lhsT_scale=scales[:, P * t : P * (t + 1)],
-                        rhs=g_words[a][:, HALF * s : HALF * (s + 1)].bitcast(FP8X4),
-                        rhs_scale=g_scales[4:, a, HALF * s : HALF * (s + 1)],
-                        start=(a == 0),
-                        stop=(a == 1),
-                    )
-            for lo in range(0, HALF, width):
-                gate = held([P, width // 4, PACK, 4], F32, f"sig{b}{s}_{lo}")
-                for u in range(width // GROUP):
-                    sig[(b, HALF * s + lo + GROUP * u)] = gate[:, GROUP // 4 * u : GROUP // 4 * (u + 1)]
-                for t in range(PACK):
+        def gates(b, first, width, tags):
+            per_bank = PACK // len(tags)
+            gate = held([P, width // 4, PACK, 4], F32, f"sig{b}_{first}", 0 if (b, first) == (1, CHUNK) else None)
+            for u in range(width // GROUP):
+                sig[(b, first + GROUP * u)] = gate[:, GROUP // 4 * u : GROUP // 4 * (u + 1)]
+            for i, tag in enumerate(tags):
+                bank = psum.tile([P, per_bank, width], F32, name="g_bank", tag=tag)
+                for e in range(per_bank):
+                    t = per_bank * i + e
+                    for a in range(2):
+                        codes, scales = wgq[(a, b)]
+                        nc.tensor.matmul_mx(
+                            bank[:, e, :],
+                            lhsT=codes[:, P * t : P * (t + 1)].bitcast(FP8X4),
+                            lhsT_scale=scales[:, P * t : P * (t + 1)],
+                            rhs=g_words[a][:, first : first + width].bitcast(FP8X4),
+                            rhs_scale=g_scales[4:, a, first : first + width],
+                            start=(a == 0),
+                            stop=(a == 1),
+                        )
+                for e in range(per_bank):
+                    t = per_bank * i + e
                     nc.scalar.activation(
                         gate[:, :, t, :],
-                        banks[t][:, lo : lo + width].rearrange("p (c e) -> p c e", e=4),
+                        bank[:, e, :].rearrange("p (c e) -> p c e", e=4),
                         ACT.Sigmoid,
                         bias=bg_sb[:, b, t : t + 1],
                     )
 
+        wide = [f"wide{i}" for i in range(4)]
         h0_codes = held([P, S], U32, "h0_codes")
         h_scales = [held([P, S], U8, f"h_scales{b}") for b in range(2)]
 
@@ -209,7 +208,7 @@ def tile_list_paged_gated_values_kernel(
 
         def project_values(g):
             b, tok = groups[g]
-            bank = psum.tile([P, PACK, GROUP], F32, name="a_bank", tag=f"value{g % 4}")
+            bank = psum.tile([P, PACK, GROUP], F32, name="a_bank", tag=f"value{g % 4}" if g < 14 else f"wide{g % 2}")
             for t in range(PACK):
                 col = PASS * b + P * t
                 nc.tensor.matmul_mx(
@@ -241,8 +240,8 @@ def tile_list_paged_gated_values_kernel(
         def quantise_h(b, first, width, hb, codes):
             nc.vector.quantize_mx(codes.bitcast(FP8X4), h_scales[b][:, first : first + width], hb[:])
 
-        gates(0, 0, HALF)
-        gates(0, 1, HALF)
+        gates(0, 0, HALF, wide)
+        gates(0, HALF, HALF, wide)
         for g in range(4):
             project_values(g)
         wg01 = round_wg(0, 1)
@@ -253,37 +252,31 @@ def tile_list_paged_gated_values_kernel(
         hb_b = gate_values(0, HALF, CHUNK)
         quantise_h(0, 0, HALF, hb_a, h0_codes[:, :HALF])
         wgq[(1, 1)] = quantise_wg(1, 1, wg11)
-        gates(1, 0, CHUNK)
+        gates(1, 0, CHUNK, wide[:2])
+        gates(1, CHUNK, CHUNK, wide[2:])
         wo0b = round_wo(0, CHUNK, CHUNK, "gpsimd", offset=10240, room=2)
         hb_c = gate_values(0, HALF + CHUNK, CHUNK, offset=8192)
         quantise_h(0, HALF, CHUNK, hb_b, h0_codes[:, HALF : HALF + CHUNK])
         quantise_wo(0, 0, CHUNK, wo0a)
         quantise_h(0, HALF + CHUNK, CHUNK, hb_c, h0_codes[:, HALF + CHUNK :])
         quantise_wo(0, CHUNK, CHUNK, wo0b)
-        gates(1, 1, HALF)
+        gates(1, HALF, HALF, wide)
         wo1b = round_wo(1, CHUNK, CHUNK, "gpsimd", offset=8256)
         wo1a = round_wo(1, 0, CHUNK, "gpsimd", offset=10304)
 
         out_rows = out.rearrange("(j p) s -> p j s", p=P)
 
-        def project(lo, width, codes, early=True):
-            kind = "wide" if width == CHUNK else "value"
-            first = 2 * (lo // width % 2)
-            banks = [psum.tile([P, 2, CHUNK], F32, name="y_bank", tag=f"{kind}{first + i}") for i in range(2)]
-            if early:
-                order = [(b, j) for b in range(2) for j in range(PACK)]
-            else:
-                order = [(b, j) for j in range(PACK) for b in (1, 0)]
-            for b, j in order:
-                mates = [o for o in order if o[1] // 2 == j // 2]
+        def project(lo, width, codes, tags):
+            banks = [psum.tile([P, 2, CHUNK], F32, name="y_bank", tag=tag) for tag in tags]
+            for j, b in [(2 * pair + e, b) for pair in range(2) for b in range(2) for e in range(2)]:
                 nc.tensor.matmul_mx(
                     banks[j // 2][:, j % 2, :width],
-                    lhsT=wo_codes[b][:, P * j : P * (j + 1)].bitcast(FP8X4),
-                    lhsT_scale=wo_scales[b][:, P * j : P * (j + 1)],
+                    lhsT=wo_codes[(b, j // 2)][:, P * (j % 2) : P * (j % 2 + 1)].bitcast(FP8X4),
+                    lhsT_scale=wo_scales[(b, j // 2)][:, P * (j % 2) : P * (j % 2 + 1)],
                     rhs=(h0_codes[:, lo : lo + width] if b == 0 else codes).bitcast(FP8X4),
                     rhs_scale=h_scales[b][:, lo : lo + width],
-                    start=(b, j) == mates[0],
-                    stop=(b, j) == mates[-1],
+                    start=(b == 0 and j % 2 == 0),
+                    stop=(b == 1 and j % 2 == 1),
                 )
             return banks
 
@@ -305,21 +298,21 @@ def tile_list_paged_gated_values_kernel(
         codes.extend(held([P, CHUNK], U32, f"h1_codes{c}") for c in range(2, 4))
         quantise_h(1, 0, CHUNK, hb_0, codes[0][:])
         quantise_wo(1, CHUNK, CHUNK, wo1b)
-        for pair, bank in enumerate(project(0, CHUNK, codes[0][:])):
+        for pair, bank in enumerate(project(0, CHUNK, codes[0][:], ("value2", "value3"))):
             store(0, CHUNK, pair, bank)
         quantise_h(1, CHUNK, CHUNK, hb_1, codes[1][:])
-        for pair, bank in enumerate(project(CHUNK, CHUNK, codes[1][:], early=False)):
+        for pair, bank in enumerate(project(CHUNK, CHUNK, codes[1][:], ("wide2", "wide3"))):
             store(CHUNK, CHUNK, pair, bank)
         hb_2 = gate_values(1, 2 * CHUNK, CHUNK, offset=8256)
         hb_3 = gate_values(1, 3 * CHUNK, GROUP, offset=12352)
         quantise_h(1, 2 * CHUNK, CHUNK, hb_2, codes[2][:])
-        banks_2 = project(2 * CHUNK, CHUNK, codes[2][:])
+        banks_2 = project(2 * CHUNK, CHUNK, codes[2][:], ("value0", "value1"))
         store(2 * CHUNK, CHUNK, 0, banks_2[0])
         hb_4 = gate_values(1, 3 * CHUNK + GROUP, GROUP, offset=13376)
         quantise_h(1, 3 * CHUNK, GROUP, hb_3, codes[3][:, :GROUP])
-        banks_3 = project(3 * CHUNK, GROUP, codes[3][:, :GROUP], early=False)
+        banks_3 = project(3 * CHUNK, GROUP, codes[3][:, :GROUP], ("wide0", "wide1"))
         quantise_h(1, 3 * CHUNK + GROUP, GROUP, hb_4, codes[3][:, GROUP:])
-        banks_4 = project(3 * CHUNK + GROUP, GROUP, codes[3][:, GROUP:])
+        banks_4 = project(3 * CHUNK + GROUP, GROUP, codes[3][:, GROUP:], ("value2", "value3"))
         store(2 * CHUNK, CHUNK, 1, banks_2[1], on_vector=True, offset=14336)
         for lo, banks in ((3 * CHUNK, banks_3), (3 * CHUNK + GROUP, banks_4)):
             store(lo, GROUP, 0, banks[0])

@@ -141,7 +141,8 @@ def tile_list_paged_gated_values_kernel(
             elif engine == "vector":
                 nc.vector.tensor_copy(dst, src)
             else:
-                nc.gpsimd.tensor_scalar(dst, src, 1.0, 0.0, MULT, ADD)
+                rows = wo_raw[b][:, :, first : first + width].rearrange("p j m -> p m j")
+                nc.gpsimd.tensor_scalar(wide.rearrange("p (m j) -> p m j", j=PACK), rows, 1.0, 0.0, MULT, ADD)
             return wide
 
         wo_codes = {(b, h): held([P, CHUNK], U32, f"wo_codes{b}{h}", 0 if (b, h) == (1, 0) else None) for b in range(2) for h in range(2)}

@@ -23,6 +23,7 @@ PASS = 512
 HALF = 512
 GROUP = 128
 CHUNK = 256
+EDGE = 64
 
 
 def tile_list_paged_gated_values_kernel(
@@ -41,32 +42,24 @@ def tile_list_paged_gated_values_kernel(
 
         idx = keep.tile([P, S // 16], U16, name="idx")
         idx2 = keep.tile([P, S // 16], U16, name="idx2")
-        v_words = [held([P, T], U32, f"v_words{a}") for a in range(2)]
+        v_words = [held([P, T], U32, "v_words0"), held([P, T], U32, "v_words1", offset=16384)]
         v_scales = held([P, T], U8, "v_scales")
         v2_words = held([P, T2], U32, "v2_words")
-        v2_scales = held([P, T2], U8, "v2_scales", offset=16384)
+        v2_scales = held([P, T2], U8, "v2_scales")
         wv_raw = held([P, 2 * H], U8, "wv_raw")
-        wv_raw_scales = held([P, H], U8, "wv_raw_scales", offset=20480)
+        wv_raw_scales = held([P, H], U8, "wv_raw_scales")
         wg_raw = [[held([P, PACK, PASS], F32, f"wg_raw{a}{b}") for b in range(2)] for a in range(2)]
         wo_raw = [held([P, PACK, N], F32, f"wo_raw{b}") for b in range(2)]
         bg_sb = held([P, 2, PACK], F32, "bg_sb")
         bo_sb = held([P, N // P], F32, "bo_sb")
-
-        g_scales = held([P, 2, S], U8, "g_scales")
+        g_scales = [held([P, S], U8, f"g_scales{a}") for a in range(2)]
         a_scales = held([P, S], U8, "a_scales")
 
-        nc.vector.memset(v_scales[:].bitcast(I32), 0)
-        nc.vector.memset(v2_scales[:].bitcast(I32), 0)
-        nc.gpsimd.memset(wv_raw_scales[:].bitcast(I32), 0)
-        nc.gpsimd.memset(g_scales[:].bitcast(I32), 0)
-        nc.gpsimd.memset(a_scales[:].bitcast(I32), 0)
+        for plane in (v_scales, v2_scales, wv_raw_scales, *g_scales, a_scales):
+            nc.vector.memset(plane[:].bitcast(I32), 0)
 
         def load_words(dst, src):
             nc.sync.dma_start(dst[:].bitcast(I32), src.rearrange("p t i -> p (t i)").bitcast(I32))
-
-        def load_scales(dst, src):
-            for r in range(4):
-                nc.sync.dma_start(dst[r:P:32, :].bitcast(I32), src[0, r:16:4, :].bitcast(I32))
 
         def load_wg(a, b):
             rows = wg[PASS * a : PASS * (a + 1), PASS * b : PASS * (b + 1)]
@@ -74,7 +67,7 @@ def tile_list_paged_gated_values_kernel(
 
         g_words = [held([P, S], U32, f"g_words{a}") for a in range(2)]
         g_picked = held([P, S], U8, "g_picked")
-        a_words = held([P, S], U32, "a_words", offset=17408)
+        a_words = held([P, S], U32, "a_words")
         a_picked = held([P, S], U8, "a_picked")
 
         def gather(dst, window, lst, pieces=1):
@@ -84,30 +77,31 @@ def tile_list_paged_gated_values_kernel(
                     dst[:, n * i : n * (i + 1)], window[:].indirect(lst[:, n // 16 * i : n // 16 * (i + 1)])
                 )
 
+        def move_gate_scales(a):
+            for r in range(4):
+                nc.sync.dma_start(
+                    g_scales[a][4 + r : P : 32, :].bitcast(I32), g_picked[8 * r + 4 * a : P : 32, :].bitcast(I32)
+                )
+
         nc.sync.dma_start(idx[:], offs)
         nc.sync.dma_start(wv_raw[:].bitcast(I32), wv_words[0].bitcast(I32))
-        for a in range(2):
-            nc.sync.dma_start(v_scales[4 * a : P : 8, :].bitcast(I32), tab_scales[a].bitcast(I32))
+        nc.sync.dma_start(v_scales[0:P:4, :].bitcast(I32), tab_scales.rearrange("a q t -> q a t").bitcast(I32))
         load_words(v_words[0], tab_words[0])
         nc.sync.dma_start(idx2[:], offs2)
         nc.sync.dma_start(v2_scales[0:P:8, :].bitcast(I32), tab2_scales[0].bitcast(I32))
+        nc.sync.dma_start(bg_sb[:], bg.rearrange("(b p t) -> p b t", b=2, t=PACK))
         load_wg(0, 0)
-        load_scales(wv_raw_scales, wv_scales)
+        for r in range(4):
+            nc.sync.dma_start(wv_raw_scales[r:P:32, :].bitcast(I32), wv_scales[0, r:16:4, :].bitcast(I32))
         load_wg(1, 0)
         gather(g_picked, v_scales, idx)
-        for q in range(4):
-            nc.sync.dma_start(
-                g_scales[32 * q + 4 : 32 * q + 8].rearrange("p a s -> p (a s)").bitcast(I32),
-                g_picked[32 * q : 32 * (q + 1) : 4, :].bitcast(I32),
-            )
+        move_gate_scales(0)
         load_words(v_words[1], tab_words[1])
-        nc.sync.dma_start(bg_sb[:], bg.rearrange("(b p t) -> p b t", b=2, t=PACK))
+        move_gate_scales(1)
         load_words(v2_words, tab2_words[0])
         gather(a_picked, v2_scales, idx2)
-        for q in range(4):
-            nc.sync.dma_start(
-                a_scales[32 * q : 32 * q + 4, :].bitcast(I32), a_picked[32 * q : 32 * (q + 1) : 8, :].bitcast(I32)
-            )
+        for r in range(4):
+            nc.sync.dma_start(a_scales[r:P:32, :].bitcast(I32), a_picked[8 * r : P : 32, :].bitcast(I32))
         load_wg(0, 1)
         load_wg(1, 1)
         for b in range(2):
@@ -115,50 +109,41 @@ def tile_list_paged_gated_values_kernel(
         with nc.allow_non_contiguous_dma(reason="one bias value a partition"):
             nc.sync.dma_start(bo_sb[:], bo.rearrange("(j p) -> p j", p=P))
 
-        def round_wg(a, b, offset=None, second=None):
+        def round_wg(a, b, offset=None, shared=None):
             wide = held([P, PACK * PASS], BF16, f"wg_bf{a}{b}", offset)
             dst = wide[:].rearrange("p (u e m j) -> p u m j e", u=2, e=2, j=PACK)
             src = wg_raw[a][b][:].rearrange("p j (m u e) -> p u m j e", u=2, e=2)
-            if second is None:
+            if shared is None:
                 nc.scalar.copy(dst, src)
             else:
-                nc.scalar.copy(dst[:, :, :64], src[:, :, :64])
-                second(dst[:, :, 64:], src[:, :, 64:])
+                nc.scalar.copy(dst[:, 0], src[:, 0])
+                if shared:
+                    nc.scalar.copy(dst[:, 1, :shared], src[:, 1, :shared])
+                nc.vector.tensor_copy(dst[:, 1, shared:], src[:, 1, shared:])
             return wide
 
-        def quantise_wg(a, b, wide):
-            codes = held([P, PASS], U32, f"wg_codes{a}{b}")
-            scales = held([P, PASS], U8, f"wg_scales{a}{b}")
+        def quantise(name, wide, offset=None):
+            width = wide.shape[1] // PACK
+            codes = held([P, width], U32, f"{name}_codes", offset)
+            scales = held([P, width], U8, f"{name}_scales")
             nc.vector.quantize_mx(codes[:].bitcast(FP8X4), scales[:], wide[:])
             return codes, scales
 
-        def round_wo(b, first, width, engine, offset=None, room=1):
-            wide = held([P, room * PACK * width], BF16, f"wo_bf{b}_{first}", offset)[:, : PACK * width]
+        def round_wo(wide, b, pair, on_scalar=False):
             dst = wide.rearrange("p (m e j) -> p m j e", e=2, j=PACK)
-            src = wo_raw[b][:, :, first : first + width].rearrange("p j (m e) -> p m j e", e=2)
-            if engine == "scalar":
+            src = wo_raw[b][:, :, CHUNK * pair : CHUNK * (pair + 1)].rearrange("p j (m e) -> p m j e", e=2)
+            if on_scalar:
                 nc.scalar.copy(dst, src)
-            elif engine == "vector":
-                nc.vector.tensor_copy(dst, src)
             else:
-                rows = wo_raw[b][:, :, first : first + width].rearrange("p j m -> p m j")
-                nc.gpsimd.tensor_scalar(wide.rearrange("p (m j) -> p m j", j=PACK), rows, 1.0, 0.0, MULT, ADD)
-            return wide
-
-        wo_codes = {(b, h): held([P, CHUNK], U32, f"wo_codes{b}{h}", 0 if (b, h) == (1, 0) else None) for b in range(2) for h in range(2)}
-        wo_scales = {(b, h): held([P, CHUNK], U8, f"wo_scales{b}{h}") for b in range(2) for h in range(2)}
-
-        def quantise_wo(b, first, width, wide):
-            key = (b, first // CHUNK)
-            nc.vector.quantize_mx(wo_codes[key][:].bitcast(FP8X4), wo_scales[key][:], wide)
+                nc.gpsimd.tensor_scalar(dst, src, 1.0, 0.0, MULT, ADD)
 
         gather(g_words[0], v_words[0], idx)
         wgq = {}
-        wgq[(0, 0)] = quantise_wg(0, 0, round_wg(0, 0))
-        wgq[(1, 0)] = quantise_wg(1, 0, round_wg(1, 0, second=nc.vector.tensor_copy))
+        wgq[(0, 0)] = quantise("wg00", round_wg(0, 0))
+        wgq[(1, 0)] = quantise("wg10", round_wg(1, 0, shared=0))
         gather(g_words[1], v_words[1], idx, pieces=2)
-        wv_codes = held([P, 2 * H], U8, "wv_codes")
-        wv_sc = held([P, H], U8, "wv_sc")
+        wv_codes = held([P, 2 * H], U8, "wv_codes", offset=16384)
+        wv_sc = held([P, H], U8, "wv_sc", offset=16384 + 2 * H)
         nc.vector.tensor_copy(
             wv_codes[:].bitcast(U16).rearrange("p (b t m) -> p b t m", b=2, t=PACK),
             wv_raw[:].bitcast(U16).rearrange("p (b m t) -> p b t m", b=2, t=PACK),
@@ -171,25 +156,25 @@ def tile_list_paged_gated_values_kernel(
 
         sig = {}
 
-        def gates(b, first, width, tags):
+        def gates(b, first, width, tags, offset=None):
             per_bank = PACK // len(tags)
-            gate = held([P, width // 4, PACK, 4], F32, f"sig{b}_{first}", 0 if (b, first) == (1, CHUNK) else None)
+            gate = held([P, width // 4, PACK, 4], F32, f"sig{b}_{first}", offset)
             for u in range(width // GROUP):
                 sig[(b, first + GROUP * u)] = gate[:, GROUP // 4 * u : GROUP // 4 * (u + 1)]
             for i, tag in enumerate(tags):
                 bank = psum.tile([P, per_bank, width], F32, name="g_bank", tag=tag)
-                for e in range(per_bank):
-                    t = per_bank * i + e
-                    for a in range(2):
-                        codes, scales = wgq[(a, b)]
+                for a in range(2):
+                    codes, scales = wgq[(a, b)]
+                    for e in range(per_bank):
+                        t = per_bank * i + e
                         nc.tensor.matmul_mx(
                             bank[:, e, :],
                             lhsT=codes[:, P * t : P * (t + 1)].bitcast(FP8X4),
                             lhsT_scale=scales[:, P * t : P * (t + 1)],
                             rhs=g_words[a][:, first : first + width].bitcast(FP8X4),
-                            rhs_scale=g_scales[4:, a, first : first + width],
-                            start=(a == 0),
-                            stop=(a == 1),
+                            rhs_scale=g_scales[a][4:, first : first + width],
+                            start=(a == 0 and e == 0),
+                            stop=(a == 1 and e == per_bank - 1),
                         )
                 for e in range(per_bank):
                     t = per_bank * i + e
@@ -200,16 +185,14 @@ def tile_list_paged_gated_values_kernel(
                         bias=bg_sb[:, b, t : t + 1],
                     )
 
-        wide = [f"wide{i}" for i in range(4)]
-        h0_codes = held([P, S], U32, "h0_codes")
-        h_scales = [held([P, S], U8, f"h_scales{b}") for b in range(2)]
-
+        wide_banks = [f"wide{i}" for i in range(4)]
         groups = [(b, tok) for b in range(2) for tok in range(0, S, GROUP)]
+        value_tags = [f"value{g % 4}" for g in range(12)] + wide_banks
         values = {}
 
         def project_values(g):
             b, tok = groups[g]
-            bank = psum.tile([P, PACK, GROUP], F32, name="a_bank", tag=f"value{g % 4}" if g < 14 else f"wide{g % 2}")
+            bank = psum.tile([P, PACK, GROUP], F32, name="a_bank", tag=value_tags[g])
             for t in range(PACK):
                 col = PASS * b + P * t
                 nc.tensor.matmul_mx(
@@ -223,8 +206,8 @@ def tile_list_paged_gated_values_kernel(
                 )
             values[groups[g]] = bank
 
-        def gate_values(b, first, width, offset=None):
-            hb = held([P, width * PACK], BF16, f"hb{b}_{first}", offset)
+        def gate_values(b, first, width, offset=None, into=None):
+            hb = held([P, width * PACK], BF16, f"hb{b}_{first}", offset) if into is None else into
             for u in range(width // GROUP):
                 tok = first + GROUP * u
                 nc.vector.tensor_tensor(
@@ -233,88 +216,127 @@ def tile_list_paged_gated_values_kernel(
                     sig[(b, tok)],
                     MULT,
                 )
-                ahead = groups.index((b, tok)) + 4
-                if ahead < len(groups):
-                    project_values(ahead)
             return hb
 
-        def quantise_h(b, first, width, hb, codes):
-            nc.vector.quantize_mx(codes.bitcast(FP8X4), h_scales[b][:, first : first + width], hb[:])
-
-        gates(0, 0, HALF, wide)
-        gates(0, HALF, HALF, wide)
-        for g in range(4):
-            project_values(g)
-        wg01 = round_wg(0, 1)
-        wg11 = round_wg(1, 1, offset=8192)
-        wo0a = round_wo(0, 0, CHUNK, "scalar")
-        hb_a = gate_values(0, 0, HALF)
-        wgq[(0, 1)] = quantise_wg(0, 1, wg01)
-        hb_b = gate_values(0, HALF, CHUNK)
-        quantise_h(0, 0, HALF, hb_a, h0_codes[:, :HALF])
-        wgq[(1, 1)] = quantise_wg(1, 1, wg11)
-        gates(1, 0, CHUNK, wide[:2])
-        gates(1, CHUNK, CHUNK, wide[2:])
-        wo0b = round_wo(0, CHUNK, CHUNK, "gpsimd", offset=10240, room=2)
-        hb_c = gate_values(0, HALF + CHUNK, CHUNK, offset=8192)
-        quantise_h(0, HALF, CHUNK, hb_b, h0_codes[:, HALF : HALF + CHUNK])
-        quantise_wo(0, 0, CHUNK, wo0a)
-        quantise_h(0, HALF + CHUNK, CHUNK, hb_c, h0_codes[:, HALF + CHUNK :])
-        quantise_wo(0, CHUNK, CHUNK, wo0b)
-        gates(1, HALF, HALF, wide)
-        wo1b = round_wo(1, CHUNK, CHUNK, "gpsimd", offset=8256)
-        wo1a = round_wo(1, 0, CHUNK, "gpsimd", offset=10304)
-
         out_rows = out.rearrange("(j p) s -> p j s", p=P)
+        hq = {}
+        woq = {}
 
-        def project(lo, width, codes, tags):
-            banks = [psum.tile([P, 2, CHUNK], F32, name="y_bank", tag=tag) for tag in tags]
-            for j, b in [(2 * pair + e, b) for pair in range(2) for b in range(2) for e in range(2)]:
+        def quantise_wo(pair, wide):
+            codes, scales = quantise(f"wo{pair}", wide, offset=20480 + 2048 * pair)
+            for b in range(2):
+                woq[(b, pair)] = (codes[:, CHUNK * b : CHUNK * (b + 1)], scales[:, CHUNK * b : CHUNK * (b + 1)])
+
+        def project(b, lo, width, pair, bank):
+            if b == 0:
+                bank = psum.tile([P, 2, CHUNK], F32, name="y_bank", tag=bank)
+            first = max(f for (bb, f) in hq if bb == b and f <= lo)
+            codes, scales = hq[(b, first)]
+            wcodes, wscales = woq[(b, pair)]
+            for e in range(2):
                 nc.tensor.matmul_mx(
-                    banks[j // 2][:, j % 2, :width],
-                    lhsT=wo_codes[(b, j // 2)][:, P * (j % 2) : P * (j % 2 + 1)].bitcast(FP8X4),
-                    lhsT_scale=wo_scales[(b, j // 2)][:, P * (j % 2) : P * (j % 2 + 1)],
-                    rhs=(h0_codes[:, lo : lo + width] if b == 0 else codes).bitcast(FP8X4),
-                    rhs_scale=h_scales[b][:, lo : lo + width],
-                    start=(b == 0 and j % 2 == 0),
-                    stop=(b == 1 and j % 2 == 1),
+                    bank[:, e, :width],
+                    lhsT=wcodes[:, P * e : P * (e + 1)].bitcast(FP8X4),
+                    lhsT_scale=wscales[:, P * e : P * (e + 1)],
+                    rhs=codes[:, lo - first : lo - first + width].bitcast(FP8X4),
+                    rhs_scale=scales[:, lo - first : lo - first + width],
+                    start=(b == 0 and e == 0),
+                    stop=(b == 1 and e == 1),
                 )
-            return banks
+            return bank
 
-        def store(lo, width, pair, bank, on_vector=False, offset=None):
-            res = held([P, 2, width], F32, f"res{lo}_{pair}", offset)
+        def project_row_block(b, j, bank):
+            if b == 0:
+                bank = psum.tile([P, HALF], F32, name="y_bank", tag=bank)
+            wcodes, wscales = woq[(b, j // 2)]
+            codes, scales = hq[(b, 0)]
+            nc.tensor.matmul_mx(
+                bank[:],
+                lhsT=wcodes[:, P * (j % 2) : P * (j % 2 + 1)].bitcast(FP8X4),
+                lhsT_scale=wscales[:, P * (j % 2) : P * (j % 2 + 1)],
+                rhs=codes[:].bitcast(FP8X4),
+                rhs_scale=scales[:],
+                start=(b == 0),
+                stop=(b == 1),
+            )
+            return bank
+
+        def store_row_block(j, bank):
+            res = held([P, HALF], F32, f"res_block{j}")
+            nc.scalar.activation(res[:], bank[:], ACT.Identity, bias=bo_sb[:, j : j + 1])
+            nc.sync.dma_start(out_rows[:, j, :HALF], res[:])
+
+        def add_bias(res, width, pair, bank, on_vector=False):
             if on_vector:
                 bias = bo_sb[:, 2 * pair : 2 * pair + 2].unsqueeze(2).to_broadcast([P, 2, width])
-                nc.vector.tensor_tensor(res[:], bank[:, :, :width], bias, ADD)
+                nc.vector.tensor_tensor(res, bank[:, :, :width], bias, ADD)
             else:
                 for e in range(2):
                     j = 2 * pair + e
                     nc.scalar.activation(res[:, e, :], bank[:, e, :width], ACT.Identity, bias=bo_sb[:, j : j + 1])
+
+        def store(lo, width, pair, bank):
+            res = held([P, 2, width], F32, f"res{lo}_{pair}")
+            add_bias(res[:], width, pair, bank)
             nc.sync.dma_start(out_rows[:, 2 * pair : 2 * pair + 2, lo : lo + width], res[:])
 
-        hb_0 = gate_values(1, 0, CHUNK, offset=12352)
-        hb_1 = gate_values(1, CHUNK, CHUNK)
-        quantise_wo(1, 0, CHUNK, wo1a)
-        codes = [held([P, CHUNK], U32, f"h1_codes{c}", offset=10304 + 1024 * c) for c in range(2)]
-        codes.extend(held([P, CHUNK], U32, f"h1_codes{c}") for c in range(2, 4))
-        quantise_h(1, 0, CHUNK, hb_0, codes[0][:])
-        quantise_wo(1, CHUNK, CHUNK, wo1b)
-        for pair, bank in enumerate(project(0, CHUNK, codes[0][:], ("value2", "value3"))):
-            store(0, CHUNK, pair, bank)
-        quantise_h(1, CHUNK, CHUNK, hb_1, codes[1][:])
-        for pair, bank in enumerate(project(CHUNK, CHUNK, codes[1][:], ("wide2", "wide3"))):
-            store(CHUNK, CHUNK, pair, bank)
-        hb_2 = gate_values(1, 2 * CHUNK, CHUNK, offset=8256)
-        hb_3 = gate_values(1, 3 * CHUNK, GROUP, offset=12352)
-        quantise_h(1, 2 * CHUNK, CHUNK, hb_2, codes[2][:])
-        banks_2 = project(2 * CHUNK, CHUNK, codes[2][:], ("value0", "value1"))
-        store(2 * CHUNK, CHUNK, 0, banks_2[0])
-        hb_4 = gate_values(1, 3 * CHUNK + GROUP, GROUP, offset=13376)
-        quantise_h(1, 3 * CHUNK, GROUP, hb_3, codes[3][:, :GROUP])
-        banks_3 = project(3 * CHUNK, GROUP, codes[3][:, :GROUP], ("wide0", "wide1"))
-        quantise_h(1, 3 * CHUNK + GROUP, GROUP, hb_4, codes[3][:, GROUP:])
-        banks_4 = project(3 * CHUNK + GROUP, GROUP, codes[3][:, GROUP:], ("value2", "value3"))
-        store(2 * CHUNK, CHUNK, 1, banks_2[1], on_vector=True, offset=14336)
-        for lo, banks in ((3 * CHUNK, banks_3), (3 * CHUNK + GROUP, banks_4)):
-            store(lo, GROUP, 0, banks[0])
-            store(lo, GROUP, 1, banks[1], on_vector=True)
+        gates(0, 0, HALF, wide_banks)
+        gates(0, HALF, HALF, wide_banks)
+        for g in range(4):
+            project_values(g)
+        wg01 = round_wg(0, 1)
+        hb = gate_values(0, 0, HALF)
+        for g in range(4, 8):
+            project_values(g)
+        hq[(0, 0)] = quantise("h0a", hb)
+        wgq[(0, 1)] = quantise("wg01", wg01)
+        wgq[(1, 1)] = quantise("wg11", round_wg(1, 1, offset=4096, shared=40))
+        wo_a = held([P, 2 * PACK * CHUNK], BF16, "wo_a_bf", 8192 - EDGE)
+        wo_b = held([P, 2 * PACK * CHUNK], BF16, "wo_b_bf", 12288)
+        round_wo(wo_b[:, : PACK * CHUNK], 0, 1, on_scalar=True)
+        gates(1, 0, CHUNK, wide_banks[:2])
+        gates(1, CHUNK, CHUNK, wide_banks[2:], offset=20480)
+        for b in range(2):
+            round_wo(wo_a[:, PACK * CHUNK * b : PACK * CHUNK * (b + 1)], b, 0)
+        round_wo(wo_b[:, PACK * CHUNK :], 1, 1)
+        hb0b = gate_values(0, HALF, HALF, offset=EDGE)
+        for g in range(8, 12):
+            project_values(g)
+        gates(1, 2 * CHUNK, CHUNK, wide_banks[:2])
+        gates(1, 3 * CHUNK, CHUNK, wide_banks[2:])
+        hb = gate_values(1, 0, HALF)
+        project_values(12)
+        project_values(13)
+        quantise_wo(0, wo_a)
+        blocks = [project_row_block(0, j, f"value{j}") for j in range(2)]
+        hq[(1, 0)] = quantise("h1a", hb)
+        for j in range(2):
+            store_row_block(j, project_row_block(1, j, blocks[j]))
+        quantise_wo(1, wo_b)
+        for j in range(2, 4):
+            store_row_block(j, project_row_block(1, j, project_row_block(0, j, f"value{j}")))
+        project_values(14)
+        project_values(15)
+        hb_c = gate_values(1, 2 * CHUNK, CHUNK, offset=6144)
+        hq[(0, HALF)] = quantise("h0b", hb0b, offset=12288)
+        banks_c = [project(0, 2 * CHUNK, CHUNK, pair, f"value{pair}") for pair in range(2)]
+        hq[(1, 2 * CHUNK)] = quantise("h1c", hb_c)
+        for pair in range(2):
+            project(1, 2 * CHUNK, CHUNK, pair, banks_c[pair])
+        hb_d = gate_values(1, 3 * CHUNK, GROUP, offset=EDGE)
+        banks_d = [project(0, 3 * CHUNK, GROUP, pair, f"value{2 + pair}") for pair in range(2)]
+        banks_e = [project(0, 3 * CHUNK + GROUP, GROUP, pair, wide_banks[pair]) for pair in range(2)]
+        hb_e = gate_values(1, 3 * CHUNK + GROUP, GROUP, offset=EDGE + 1024)
+        hq[(1, 3 * CHUNK)] = quantise("h1d", hb_d)
+        for pair in range(2):
+            project(1, 3 * CHUNK, GROUP, pair, banks_d[pair])
+        hq[(1, 3 * CHUNK + GROUP)] = quantise("h1e", hb_e)
+        for pair in range(2):
+            project(1, 3 * CHUNK + GROUP, GROUP, pair, banks_e[pair])
+        for pair in range(2):
+            store(2 * CHUNK, CHUNK, pair, banks_c[pair])
+        for pair in range(2):
+            res = held([P, 2, CHUNK], F32, f"res_last{pair}")
+            for i, banks in enumerate((banks_d, banks_e)):
+                add_bias(res[:, :, GROUP * i : GROUP * (i + 1)], GROUP, pair, banks[pair], on_vector=(pair == 1))
+            nc.sync.dma_start(out_rows[:, 2 * pair : 2 * pair + 2, 3 * CHUNK :], res[:])

@@ -42,7 +42,7 @@ def tile_list_paged_gated_values_kernel(
 
         idx = keep.tile([P, S // 16], U16, name="idx")
         idx2 = keep.tile([P, S // 16], U16, name="idx2")
-        v_words = [held([P, T], U32, "v_words0"), held([P, T], U32, "v_words1", offset=16384)]
+        v_words = [held([P, T], U32, "v_words0"), held([P, T], U32, "v_words1")]
         v_scales = held([P, T], U8, "v_scales")
         v2_words = held([P, T2], U32, "v2_words")
         v2_scales = held([P, T2], U8, "v2_scales")
@@ -66,7 +66,7 @@ def tile_list_paged_gated_values_kernel(
             nc.sync.dma_start(wg_raw[a][b][:], rows.rearrange("(p j) c -> p j c", j=PACK))
 
         g_words = [held([P, S], U32, f"g_words{a}") for a in range(2)]
-        g_picked = held([P, S], U8, "g_picked")
+        g_picked = held([P, S], U8, "g_picked", offset=49152)
         a_words = held([P, S], U32, "a_words")
         a_picked = held([P, S], U8, "a_picked")
 
@@ -129,9 +129,10 @@ def tile_list_paged_gated_values_kernel(
             nc.vector.quantize_mx(codes[:].bitcast(FP8X4), scales[:], wide[:])
             return codes, scales
 
-        def round_wo(wide, b, pair, on_scalar=False):
+        def round_wo(wide, b, first, on_scalar=False):
+            cols = wo_raw[b][:, :, first : first + wide.shape[1] // PACK]
             dst = wide.rearrange("p (m e j) -> p m j e", e=2, j=PACK)
-            src = wo_raw[b][:, :, CHUNK * pair : CHUNK * (pair + 1)].rearrange("p j (m e) -> p m j e", e=2)
+            src = cols.rearrange("p j (m e) -> p m j e", e=2)
             if on_scalar:
                 nc.scalar.copy(dst, src)
             else:
@@ -142,8 +143,8 @@ def tile_list_paged_gated_values_kernel(
         wgq[(0, 0)] = quantise("wg00", round_wg(0, 0))
         wgq[(1, 0)] = quantise("wg10", round_wg(1, 0, shared=0))
         gather(g_words[1], v_words[1], idx, pieces=2)
-        wv_codes = held([P, 2 * H], U8, "wv_codes", offset=16384)
-        wv_sc = held([P, H], U8, "wv_sc", offset=16384 + 2 * H)
+        wv_codes = held([P, 2 * H], U8, "wv_codes", offset=49152 + EDGE - 2 * H)
+        wv_sc = held([P, H], U8, "wv_sc", offset=49152 + EDGE)
         nc.vector.tensor_copy(
             wv_codes[:].bitcast(U16).rearrange("p (b t m) -> p b t m", b=2, t=PACK),
             wv_raw[:].bitcast(U16).rearrange("p (b m t) -> p b t m", b=2, t=PACK),
@@ -204,15 +205,21 @@ def tile_list_paged_gated_values_kernel(
                     start=True,
                     stop=True,
                 )
-            values[groups[g]] = bank
+            values[groups[g]] = bank[:].rearrange("p t (c e) -> p c t e", e=4)
 
-        def gate_values(b, first, width, offset=None, into=None):
-            hb = held([P, width * PACK], BF16, f"hb{b}_{first}", offset) if into is None else into
+        def copy_values(g):
+            plain = held([P, GROUP // 4, PACK, 4], F32, f"a_plain{g}")
+            nc.scalar.copy(plain[:], values[groups[g]])
+            values[groups[g]] = plain[:]
+
+        def gate_values(b, first, width, offset=None, on_gpsimd=None):
+            hb = held([P, width * PACK], BF16, f"hb{b}_{first}", offset)
             for u in range(width // GROUP):
                 tok = first + GROUP * u
-                nc.vector.tensor_tensor(
+                engine = nc.gpsimd if tok == on_gpsimd else nc.vector
+                engine.tensor_tensor(
                     hb[:, PACK * GROUP * u : PACK * GROUP * (u + 1)].rearrange("p (c e t) -> p c t e", e=4, t=PACK),
-                    values[(b, tok)][:].rearrange("p t (c e) -> p c t e", e=4),
+                    values[(b, tok)],
                     sig[(b, tok)],
                     MULT,
                 )
@@ -284,26 +291,29 @@ def tile_list_paged_gated_values_kernel(
         gates(0, HALF, HALF, wide_banks)
         for g in range(4):
             project_values(g)
-        wg01 = round_wg(0, 1)
-        hb = gate_values(0, 0, HALF)
+        copy_values(0)
+        wg01 = round_wg(0, 1, offset=24576)
+        hb = gate_values(0, 0, HALF, on_gpsimd=0)
         for g in range(4, 8):
             project_values(g)
-        hq[(0, 0)] = quantise("h0a", hb)
+        hb_fifth = gate_values(0, HALF, GROUP)
         wgq[(0, 1)] = quantise("wg01", wg01)
-        wgq[(1, 1)] = quantise("wg11", round_wg(1, 1, offset=4096, shared=40))
-        wo_a = held([P, 2 * PACK * CHUNK], BF16, "wo_a_bf", 8192 - EDGE)
+        wg11 = round_wg(1, 1, offset=40960 - EDGE, shared=32)
+        hq[(0, 0)] = quantise("h0a", hb, offset=24576)
+        wgq[(1, 1)] = quantise("wg11", wg11)
+        wo_a = held([P, 2 * PACK * CHUNK], BF16, "wo_a_bf", 36864)
         wo_b = held([P, 2 * PACK * CHUNK], BF16, "wo_b_bf", 12288)
-        round_wo(wo_b[:, : PACK * CHUNK], 0, 1, on_scalar=True)
-        gates(1, 0, CHUNK, wide_banks[:2])
-        gates(1, CHUNK, CHUNK, wide_banks[2:], offset=20480)
-        for b in range(2):
-            round_wo(wo_a[:, PACK * CHUNK * b : PACK * CHUNK * (b + 1)], b, 0)
-        round_wo(wo_b[:, PACK * CHUNK :], 1, 1)
-        hb0b = gate_values(0, HALF, HALF, offset=EDGE)
+        round_wo(wo_b[:, : PACK * CHUNK], 0, CHUNK, on_scalar=True)
+        gates(1, 0, CHUNK, wide_banks[:2], offset=20480)
+        gates(1, CHUNK, CHUNK, wide_banks[2:])
+        round_wo(wo_a[:, : PACK * CHUNK], 0, 0)
+        round_wo(wo_a[:, PACK * CHUNK :], 1, 0)
+        round_wo(wo_b[:, PACK * CHUNK : PACK * (CHUNK + GROUP)], 1, CHUNK)
+        round_wo(wo_b[:, PACK * (CHUNK + GROUP) :], 1, CHUNK + GROUP, on_scalar=True)
+        hb0b = gate_values(0, HALF + GROUP, 3 * GROUP, offset=40960)
         for g in range(8, 12):
             project_values(g)
-        gates(1, 2 * CHUNK, CHUNK, wide_banks[:2])
-        gates(1, 3 * CHUNK, CHUNK, wide_banks[2:])
+        gates(1, HALF, HALF, wide_banks)
         hb = gate_values(1, 0, HALF)
         project_values(12)
         project_values(13)
@@ -317,16 +327,20 @@ def tile_list_paged_gated_values_kernel(
             store_row_block(j, project_row_block(1, j, project_row_block(0, j, f"value{j}")))
         project_values(14)
         project_values(15)
-        hb_c = gate_values(1, 2 * CHUNK, CHUNK, offset=6144)
-        hq[(0, HALF)] = quantise("h0b", hb0b, offset=12288)
+        hb_c = gate_values(1, 2 * CHUNK, CHUNK, offset=36864)
+        codes = held([P, HALF], U32, "h0b_codes", 12288)
+        scales = held([P, HALF], U8, "h0b_scales")
+        nc.vector.quantize_mx(codes[:, GROUP:].bitcast(FP8X4), scales[:, GROUP:], hb0b[:])
+        nc.vector.quantize_mx(codes[:, :GROUP].bitcast(FP8X4), scales[:, :GROUP], hb_fifth[:])
+        hq[(0, HALF)] = (codes, scales)
         banks_c = [project(0, 2 * CHUNK, CHUNK, pair, f"value{pair}") for pair in range(2)]
         hq[(1, 2 * CHUNK)] = quantise("h1c", hb_c)
         for pair in range(2):
             project(1, 2 * CHUNK, CHUNK, pair, banks_c[pair])
-        hb_d = gate_values(1, 3 * CHUNK, GROUP, offset=EDGE)
+        hb_d = gate_values(1, 3 * CHUNK, GROUP, offset=40960)
         banks_d = [project(0, 3 * CHUNK, GROUP, pair, f"value{2 + pair}") for pair in range(2)]
         banks_e = [project(0, 3 * CHUNK + GROUP, GROUP, pair, wide_banks[pair]) for pair in range(2)]
-        hb_e = gate_values(1, 3 * CHUNK + GROUP, GROUP, offset=EDGE + 1024)
+        hb_e = gate_values(1, 3 * CHUNK + GROUP, GROUP, offset=40960 + 1024)
         hq[(1, 3 * CHUNK)] = quantise("h1d", hb_d)
         for pair in range(2):
             project(1, 3 * CHUNK, GROUP, pair, banks_d[pair])

@@ -284,7 +284,7 @@ def tile_list_paged_gated_values_kernel(
 
         def store(lo, width, pair, bank):
             res = held([P, 2, width], F32, f"res{lo}_{pair}")
-            add_bias(res[:], width, pair, bank)
+            add_bias(res[:], width, pair, bank, on_vector=(pair == 1))
             nc.sync.dma_start(out_rows[:, 2 * pair : 2 * pair + 2, lo : lo + width], res[:])
 
         gates(0, 0, HALF, wide_banks)
@@ -296,7 +296,7 @@ def tile_list_paged_gated_values_kernel(
         hb = gate_values(0, 0, HALF, on_gpsimd=0)
         for g in range(4, 8):
             project_values(g)
-        hb_fifth = gate_values(0, HALF, GROUP)
+        hb_mid = gate_values(0, HALF, CHUNK)
         wgq[(0, 1)] = quantise("wg01", wg01)
         wg11 = round_wg(1, 1, offset=40960 - EDGE, shared=32)
         hq[(0, 0)] = quantise("h0a", hb, offset=24576)
@@ -310,7 +310,12 @@ def tile_list_paged_gated_values_kernel(
         round_wo(wo_a[:, PACK * CHUNK :], 1, 0)
         round_wo(wo_b[:, PACK * CHUNK : PACK * (CHUNK + GROUP)], 1, CHUNK)
         round_wo(wo_b[:, PACK * (CHUNK + GROUP) :], 1, CHUNK + GROUP, on_scalar=True)
-        hb0b = gate_values(0, HALF + GROUP, 3 * GROUP, offset=40960)
+        hb_end = gate_values(0, HALF + CHUNK, CHUNK, offset=40960)
+        codes = held([P, HALF], U32, "h0b_codes", 40960 + 4096 - 2 * EDGE)
+        scales = held([P, HALF], U8, "h0b_scales")
+        nc.vector.quantize_mx(codes[:, :CHUNK].bitcast(FP8X4), scales[:, :CHUNK], hb_mid[:])
+        nc.vector.quantize_mx(codes[:, CHUNK:].bitcast(FP8X4), scales[:, CHUNK:], hb_end[:])
+        hq[(0, HALF)] = (codes, scales)
         for g in range(8, 12):
             project_values(g)
         gates(1, HALF, HALF, wide_banks)
@@ -328,19 +333,14 @@ def tile_list_paged_gated_values_kernel(
         project_values(14)
         project_values(15)
         hb_c = gate_values(1, 2 * CHUNK, CHUNK, offset=36864)
-        codes = held([P, HALF], U32, "h0b_codes", 12288)
-        scales = held([P, HALF], U8, "h0b_scales")
-        nc.vector.quantize_mx(codes[:, GROUP:].bitcast(FP8X4), scales[:, GROUP:], hb0b[:])
-        nc.vector.quantize_mx(codes[:, :GROUP].bitcast(FP8X4), scales[:, :GROUP], hb_fifth[:])
-        hq[(0, HALF)] = (codes, scales)
         banks_c = [project(0, 2 * CHUNK, CHUNK, pair, f"value{pair}") for pair in range(2)]
         hq[(1, 2 * CHUNK)] = quantise("h1c", hb_c)
         for pair in range(2):
             project(1, 2 * CHUNK, CHUNK, pair, banks_c[pair])
-        hb_d = gate_values(1, 3 * CHUNK, GROUP, offset=40960)
+        hb_d = gate_values(1, 3 * CHUNK, GROUP, offset=12288)
         banks_d = [project(0, 3 * CHUNK, GROUP, pair, f"value{2 + pair}") for pair in range(2)]
         banks_e = [project(0, 3 * CHUNK + GROUP, GROUP, pair, wide_banks[pair]) for pair in range(2)]
-        hb_e = gate_values(1, 3 * CHUNK + GROUP, GROUP, offset=40960 + 1024)
+        hb_e = gate_values(1, 3 * CHUNK + GROUP, GROUP, offset=12288 + 1024)
         hq[(1, 3 * CHUNK)] = quantise("h1d", hb_d)
         for pair in range(2):
             project(1, 3 * CHUNK, GROUP, pair, banks_d[pair])
@@ -349,8 +349,9 @@ def tile_list_paged_gated_values_kernel(
             project(1, 3 * CHUNK + GROUP, GROUP, pair, banks_e[pair])
         for pair in range(2):
             store(2 * CHUNK, CHUNK, pair, banks_c[pair])
-        for pair in range(2):
-            res = held([P, 2, CHUNK], F32, f"res_last{pair}")
-            for i, banks in enumerate((banks_d, banks_e)):
-                add_bias(res[:, :, GROUP * i : GROUP * (i + 1)], GROUP, pair, banks[pair], on_vector=(pair == 1))
-            nc.sync.dma_start(out_rows[:, 2 * pair : 2 * pair + 2, 3 * CHUNK :], res[:])
+        for i, banks in enumerate((banks_d, banks_e)):
+            lo = 3 * CHUNK + GROUP * i
+            res = held([P, N // P, GROUP], F32, f"res_last{i}")
+            for pair in range(2):
+                add_bias(res[:, 2 * pair : 2 * pair + 2, :], GROUP, pair, banks[pair], on_vector=(pair == 1))
+            nc.sync.dma_start(out_rows[:, :, lo : lo + GROUP], res[:])

@@ -48,7 +48,9 @@ def tile_list_paged_gated_values_kernel(
         v2_scales = held([P, T2], U8, "v2_scales")
         wv_raw = held([P, 2 * H], U8, "wv_raw")
         wv_raw_scales = held([P, H], U8, "wv_raw_scales")
-        wg_raw = [[held([P, PACK, PASS], F32, f"wg_raw{a}{b}") for b in range(2)] for a in range(2)]
+        wg_raw = [
+            [held([P, PACK, PASS], F32, f"wg_raw{a}{b}", 0 if a + b == 2 else None) for b in range(2)] for a in range(2)
+        ]
         wo_raw = [held([P, PACK, N], F32, f"wo_raw{b}") for b in range(2)]
         bg_sb = held([P, 2, PACK], F32, "bg_sb")
         bo_sb = held([P, N // P], F32, "bo_sb")
@@ -296,11 +298,12 @@ def tile_list_paged_gated_values_kernel(
         hb = gate_values(0, 0, HALF, on_gpsimd=0)
         for g in range(4, 8):
             project_values(g)
-        hb_mid = gate_values(0, HALF, CHUNK)
+        hb_mid = gate_values(0, HALF, CHUNK, offset=36864)
         wgq[(0, 1)] = quantise("wg01", wg01)
         wg11 = round_wg(1, 1, offset=40960 - EDGE, shared=32)
         hq[(0, 0)] = quantise("h0a", hb, offset=24576)
         wgq[(1, 1)] = quantise("wg11", wg11)
+        hq[(0, HALF)] = quantise("h0b", hb_mid, offset=0)
         wo_a = held([P, 2 * PACK * CHUNK], BF16, "wo_a_bf", 36864)
         wo_b = held([P, 2 * PACK * CHUNK], BF16, "wo_b_bf", 12288)
         round_wo(wo_b[:, : PACK * CHUNK], 0, CHUNK, on_scalar=True)
@@ -311,15 +314,10 @@ def tile_list_paged_gated_values_kernel(
         round_wo(wo_b[:, PACK * CHUNK : PACK * (CHUNK + GROUP)], 1, CHUNK)
         round_wo(wo_b[:, PACK * (CHUNK + GROUP) :], 1, CHUNK + GROUP, on_scalar=True)
         hb_end = gate_values(0, HALF + CHUNK, CHUNK, offset=40960)
-        codes = held([P, HALF], U32, "h0b_codes", 40960 + 4096 - 2 * EDGE)
-        scales = held([P, HALF], U8, "h0b_scales")
-        nc.vector.quantize_mx(codes[:, :CHUNK].bitcast(FP8X4), scales[:, :CHUNK], hb_mid[:])
-        nc.vector.quantize_mx(codes[:, CHUNK:].bitcast(FP8X4), scales[:, CHUNK:], hb_end[:])
-        hq[(0, HALF)] = (codes, scales)
         for g in range(8, 12):
             project_values(g)
         gates(1, HALF, HALF, wide_banks)
-        hb = gate_values(1, 0, HALF)
+        hb = gate_values(1, 0, HALF, offset=8192)
         project_values(12)
         project_values(13)
         quantise_wo(0, wo_a)
@@ -334,6 +332,7 @@ def tile_list_paged_gated_values_kernel(
         project_values(15)
         hb_c = gate_values(1, 2 * CHUNK, CHUNK, offset=36864)
         banks_c = [project(0, 2 * CHUNK, CHUNK, pair, f"value{pair}") for pair in range(2)]
+        hq[(0, HALF + CHUNK)] = quantise("h0c", hb_end, offset=8192)
         hq[(1, 2 * CHUNK)] = quantise("h1c", hb_c)
         for pair in range(2):
             project(1, 2 * CHUNK, CHUNK, pair, banks_c[pair])

from contextlib import ExitStack

import concourse.mybir as mybir

K, K2, H, N, T, T2, S = 1024, 512, 1024, 512, 2048, 4096, 1024
FLOPS = 2 * S * (K * H + K2 * H + H * N)

F32 = mybir.dt.float32
BF16 = mybir.dt.bfloat16
I32 = mybir.dt.int32
U32 = mybir.dt.uint32
U16 = mybir.dt.uint16
U8 = mybir.dt.uint8
FP8X4 = mybir.dt.float8_e4m3fn_x4
FP4X4 = mybir.dt.float4_e2m1fn_x4
ACT = mybir.ActivationFunctionType
MULT = mybir.AluOpType.mult
ADD = mybir.AluOpType.add

P = 128
PACK = 4
PASS = 512
HALF = 512
GROUP = 128
CHUNK = 256
EDGE = 64


def tile_list_paged_gated_values_kernel(
    tc, tab_words, tab_scales, offs, tab2_words, tab2_scales, offs2, wg, bg, wv_words, wv_scales, wo, bo, out
):
    nc = tc.nc
    with ExitStack() as ctx:
        keep = ctx.enter_context(tc.tile_pool(name="keep", bufs=1))
        late = ctx.enter_context(tc.tile_pool(name="late", bufs=1))
        psum = ctx.enter_context(tc.psum_pool(name="psum", bufs=1))

        def held(shape, dtype, name, offset=None):
            if offset is None:
                return keep.tile(shape, dtype, name=name, align_bytes=64)
            return late.tile(shape, dtype, name=name, offset=offset, align_bytes=64)

        idx = keep.tile([P, S // 16], U16, name="idx")
        idx2 = keep.tile([P, S // 16], U16, name="idx2")
        v_words = [held([P, T], U32, "v_words0"), held([P, T], U32, "v_words1")]
        v_scales = held([P, T], U8, "v_scales")
        v2_words = held([P, T2], U32, "v2_words")
        v2_scales = held([P, T2], U8, "v2_scales")
        wv_raw = held([P, 2 * H], U8, "wv_raw")
        wv_raw_scales = held([P, H], U8, "wv_raw_scales")
        wg_raw = [
            [held([P, PACK, PASS], F32, f"wg_raw{a}{b}", 0 if a + b == 2 else None) for b in range(2)] for a in range(2)
        ]
        wo_raw = [held([P, PACK, N], F32, f"wo_raw{b}") for b in range(2)]
        bg_sb = held([P, 2, PACK], F32, "bg_sb")
        bo_sb = held([P, N // P], F32, "bo_sb")
        g_scales = [held([P, S], U8, f"g_scales{a}") for a in range(2)]
        a_scales = held([P, S], U8, "a_scales")

        for plane in (v_scales, v2_scales, wv_raw_scales, *g_scales, a_scales):
            nc.vector.memset(plane[:].bitcast(I32), 0)

        def load_words(dst, src):
            nc.sync.dma_start(dst[:].bitcast(I32), src.rearrange("p t i -> p (t i)").bitcast(I32))

        def load_wg(a, b):
            rows = wg[PASS * a : PASS * (a + 1), PASS * b : PASS * (b + 1)]
            nc.sync.dma_start(wg_raw[a][b][:], rows.rearrange("(p j) c -> p j c", j=PACK))

        g_words = [held([P, S], U32, f"g_words{a}") for a in range(2)]
        g_picked = held([P, S], U8, "g_picked", offset=49152)
        a_words = held([P, S], U32, "a_words")
        a_picked = held([P, S], U8, "a_picked")

        def gather(dst, window, lst, pieces=1):
            n = S // pieces
            for i in range(pieces):
                nc.vector.tensor_copy(
                    dst[:, n * i : n * (i + 1)], window[:].indirect(lst[:, n // 16 * i : n // 16 * (i + 1)])
                )

        def move_gate_scales(a):
            for r in range(4):
                nc.sync.dma_start(
                    g_scales[a][4 + r : P : 32, :].bitcast(I32), g_picked[8 * r + 4 * a : P : 32, :].bitcast(I32)
                )

        nc.sync.dma_start(idx[:], offs)
        nc.sync.dma_start(wv_raw[:].bitcast(I32), wv_words[0].bitcast(I32))
        nc.sync.dma_start(v_scales[0:P:4, :].bitcast(I32), tab_scales.rearrange("a q t -> q a t").bitcast(I32))
        load_words(v_words[0], tab_words[0])
        nc.sync.dma_start(idx2[:], offs2)
        nc.sync.dma_start(v2_scales[0:P:8, :].bitcast(I32), tab2_scales[0].bitcast(I32))
        nc.sync.dma_start(bg_sb[:], bg.rearrange("(b p t) -> p b t", b=2, t=PACK))
        load_wg(0, 0)
        for r in range(4):
            nc.sync.dma_start(wv_raw_scales[r:P:32, :].bitcast(I32), wv_scales[0, r:16:4, :].bitcast(I32))
        load_wg(1, 0)
        gather(g_picked, v_scales, idx)
        move_gate_scales(0)
        load_words(v_words[1], tab_words[1])
        move_gate_scales(1)
        load_words(v2_words, tab2_words[0])
        gather(a_picked, v2_scales, idx2)
        for r in range(4):
            nc.sync.dma_start(a_scales[r:P:32, :].bitcast(I32), a_picked[8 * r : P : 32, :].bitcast(I32))
        load_wg(0, 1)
        load_wg(1, 1)
        for b in range(2):
            nc.sync.dma_start(wo_raw[b][:], wo[PASS * b : PASS * (b + 1), :].rearrange("(p j) n -> p j n", j=PACK))
        with nc.allow_non_contiguous_dma(reason="one bias value a partition"):
            nc.sync.dma_start(bo_sb[:], bo.rearrange("(j p) -> p j", p=P))

        def round_wg(a, b, offset=None, shared=None):
            wide = held([P, PACK * PASS], BF16, f"wg_bf{a}{b}", offset)
            dst = wide[:].rearrange("p (u e m j) -> p u m j e", u=2, e=2, j=PACK)
            src = wg_raw[a][b][:].rearrange("p j (m u e) -> p u m j e", u=2, e=2)
            if shared is None:
                nc.scalar.copy(dst, src)
            else:
                nc.scalar.copy(dst[:, 0], src[:, 0])
                if shared:
                    nc.scalar.copy(dst[:, 1, :shared], src[:, 1, :shared])
                nc.vector.tensor_copy(dst[:, 1, shared:], src[:, 1, shared:])
            return wide

        def quantise(name, wide, offset=None):
            width = wide.shape[1] // PACK
            codes = held([P, width], U32, f"{name}_codes", offset)
            scales = held([P, width], U8, f"{name}_scales")
            nc.vector.quantize_mx(codes[:].bitcast(FP8X4), scales[:], wide[:])
            return codes, scales

        def round_wo(wide, b, first, on_scalar=False):
            cols = wo_raw[b][:, :, first : first + wide.shape[1] // PACK]
            dst = wide.rearrange("p (m e j) -> p m j e", e=2, j=PACK)
            src = cols.rearrange("p j (m e) -> p m j e", e=2)
            if on_scalar:
                nc.scalar.copy(dst, src)
            else:
                nc.gpsimd.tensor_scalar(dst, src, 1.0, 0.0, MULT, ADD)

        gather(g_words[0], v_words[0], idx)
        wgq = {}
        wgq[(0, 0)] = quantise("wg00", round_wg(0, 0))
        wgq[(1, 0)] = quantise("wg10", round_wg(1, 0, shared=0))
        gather(g_words[1], v_words[1], idx, pieces=2)
        wv_codes = held([P, 2 * H], U8, "wv_codes", offset=49152 + EDGE - 2 * H)
        wv_sc = held([P, H], U8, "wv_sc", offset=49152 + EDGE)
        nc.vector.tensor_copy(
            wv_codes[:].bitcast(U16).rearrange("p (b t m) -> p b t m", b=2, t=PACK),
            wv_raw[:].bitcast(U16).rearrange("p (b m t) -> p b t m", b=2, t=PACK),
        )
        nc.vector.tensor_copy(
            wv_sc[:].rearrange("p (b t m) -> p b t m", b=2, t=PACK),
            wv_raw_scales[:].rearrange("p (b m t) -> p b t m", b=2, t=PACK),
        )
        gather(a_words, v2_words, idx2, pieces=2)

        sig = {}

        def gates(b, first, width, tags, offset=None):
            per_bank = PACK // len(tags)
            gate = held([P, width // 4, PACK, 4], F32, f"sig{b}_{first}", offset)
            for u in range(width // GROUP):
                sig[(b, first + GROUP * u)] = gate[:, GROUP // 4 * u : GROUP // 4 * (u + 1)]
            for i, tag in enumerate(tags):
                bank = psum.tile([P, per_bank, width], F32, name="g_bank", tag=tag)
                for a in range(2):
                    codes, scales = wgq[(a, b)]
                    for e in range(per_bank):
                        t = per_bank * i + e
                        nc.tensor.matmul_mx(
                            bank[:, e, :],
                            lhsT=codes[:, P * t : P * (t + 1)].bitcast(FP8X4),
                            lhsT_scale=scales[:, P * t : P * (t + 1)],
                            rhs=g_words[a][:, first : first + width].bitcast(FP8X4),
                            rhs_scale=g_scales[a][4:, first : first + width],
                            start=(a == 0 and e == 0),
                            stop=(a == 1 and e == per_bank - 1),
                        )
                for e in range(per_bank):
                    t = per_bank * i + e
                    nc.scalar.activation(
                        gate[:, :, t, :],
                        bank[:, e, :].rearrange("p (c e) -> p c e", e=4),
                        ACT.Sigmoid,
                        bias=bg_sb[:, b, t : t + 1],
                    )

        wide_banks = [f"wide{i}" for i in range(4)]
        groups = [(b, tok) for b in range(2) for tok in range(0, S, GROUP)]
        value_tags = [f"value{g % 4}" for g in range(12)] + wide_banks
        values = {}

        def project_values(g):
            b, tok = groups[g]
            bank = psum.tile([P, PACK, GROUP], F32, name="a_bank", tag=value_tags[g])
            for t in range(PACK):
                col = PASS * b + P * t
                nc.tensor.matmul_mx(
                    bank[:, t, :],
                    lhsT=wv_codes[:, 2 * col : 2 * (col + P)].bitcast(FP4X4),
                    lhsT_scale=wv_sc[:, col : col + P],
                    rhs=a_words[:, tok : tok + GROUP].bitcast(FP8X4),
                    rhs_scale=a_scales[:, tok : tok + GROUP],
                    start=True,
                    stop=True,
                )
            values[groups[g]] = bank[:].rearrange("p t (c e) -> p c t e", e=4)

        def copy_values(g):
            plain = held([P, GROUP // 4, PACK, 4], F32, f"a_plain{g}")
            nc.scalar.copy(plain[:], values[groups[g]])
            values[groups[g]] = plain[:]

        def gate_values(b, first, width, offset=None, on_gpsimd=None):
            hb = held([P, width * PACK], BF16, f"hb{b}_{first}", offset)
            for u in range(width // GROUP):
                tok = first + GROUP * u
                engine = nc.gpsimd if tok == on_gpsimd else nc.vector
                engine.tensor_tensor(
                    hb[:, PACK * GROUP * u : PACK * GROUP * (u + 1)].rearrange("p (c e t) -> p c t e", e=4, t=PACK),
                    values[(b, tok)],
                    sig[(b, tok)],
                    MULT,
                )
            return hb

        out_rows = out.rearrange("(j p) s -> p j s", p=P)
        hq = {}
        woq = {}

        def quantise_wo(pair, wide):
            codes, scales = quantise(f"wo{pair}", wide, offset=20480 + 2048 * pair)
            for b in range(2):
                woq[(b, pair)] = (codes[:, CHUNK * b : CHUNK * (b + 1)], scales[:, CHUNK * b : CHUNK * (b + 1)])

        def project(b, lo, width, pair, bank):
            if b == 0:
                bank = psum.tile([P, 2, CHUNK], F32, name="y_bank", tag=bank)
            first = max(f for (bb, f) in hq if bb == b and f <= lo)
            codes, scales = hq[(b, first)]
            wcodes, wscales = woq[(b, pair)]
            for e in range(2):
                nc.tensor.matmul_mx(
                    bank[:, e, :width],
                    lhsT=wcodes[:, P * e : P * (e + 1)].bitcast(FP8X4),
                    lhsT_scale=wscales[:, P * e : P * (e + 1)],
                    rhs=codes[:, lo - first : lo - first + width].bitcast(FP8X4),
                    rhs_scale=scales[:, lo - first : lo - first + width],
                    start=(b == 0 and e == 0),
                    stop=(b == 1 and e == 1),
                )
            return bank

        def project_row_block(b, j, bank):
            if b == 0:
                bank = psum.tile([P, HALF], F32, name="y_bank", tag=bank)
            wcodes, wscales = woq[(b, j // 2)]
            codes, scales = hq[(b, 0)]
            nc.tensor.matmul_mx(
                bank[:],
                lhsT=wcodes[:, P * (j % 2) : P * (j % 2 + 1)].bitcast(FP8X4),
                lhsT_scale=wscales[:, P * (j % 2) : P * (j % 2 + 1)],
                rhs=codes[:].bitcast(FP8X4),
                rhs_scale=scales[:],
                start=(b == 0),
                stop=(b == 1),
            )
            return bank

        def store_row_block(j, bank):
            res = held([P, HALF], F32, f"res_block{j}")
            nc.scalar.activation(res[:], bank[:], ACT.Identity, bias=bo_sb[:, j : j + 1])
            nc.sync.dma_start(out_rows[:, j, :HALF], res[:])

        def add_bias(res, width, pair, bank, on_vector=False):
            if on_vector:
                bias = bo_sb[:, 2 * pair : 2 * pair + 2].unsqueeze(2).to_broadcast([P, 2, width])
                nc.vector.tensor_tensor(res, bank[:, :, :width], bias, ADD)
            else:
                for e in range(2):
                    j = 2 * pair + e
                    nc.scalar.activation(res[:, e, :], bank[:, e, :width], ACT.Identity, bias=bo_sb[:, j : j + 1])

        def store(lo, width, pair, bank):
            res = held([P, 2, width], F32, f"res{lo}_{pair}")
            add_bias(res[:], width, pair, bank, on_vector=(pair == 1))
            nc.sync.dma_start(out_rows[:, 2 * pair : 2 * pair + 2, lo : lo + width], res[:])

        gates(0, 0, HALF, wide_banks)
        gates(0, HALF, HALF, wide_banks)
        for g in range(4):
            project_values(g)
        copy_values(0)
        wg01 = round_wg(0, 1, offset=24576)
        hb = gate_values(0, 0, HALF, on_gpsimd=0)
        for g in range(4, 8):
            project_values(g)
        hb_mid = gate_values(0, HALF, CHUNK, offset=36864)
        wgq[(0, 1)] = quantise("wg01", wg01)
        wg11 = round_wg(1, 1, offset=40960 - EDGE, shared=32)
        hq[(0, 0)] = quantise("h0a", hb, offset=24576)
        wgq[(1, 1)] = quantise("wg11", wg11)
        hq[(0, HALF)] = quantise("h0b", hb_mid, offset=0)
        wo_a = held([P, 2 * PACK * CHUNK], BF16, "wo_a_bf", 36864)
        wo_b = held([P, 2 * PACK * CHUNK], BF16, "wo_b_bf", 12288)
        round_wo(wo_b[:, : PACK * CHUNK], 0, CHUNK, on_scalar=True)
        gates(1, 0, CHUNK, wide_banks[:2], offset=20480)
        gates(1, CHUNK, CHUNK, wide_banks[2:])
        round_wo(wo_a[:, : PACK * CHUNK], 0, 0)
        round_wo(wo_a[:, PACK * CHUNK :], 1, 0)
        round_wo(wo_b[:, PACK * CHUNK : PACK * (CHUNK + GROUP)], 1, CHUNK)
        round_wo(wo_b[:, PACK * (CHUNK + GROUP) :], 1, CHUNK + GROUP, on_scalar=True)
        hb_end = gate_values(0, HALF + CHUNK, CHUNK, offset=40960)
        for g in range(8, 12):
            project_values(g)
        gates(1, HALF, HALF, wide_banks)
        hb = gate_values(1, 0, HALF, offset=8192)
        project_values(12)
        project_values(13)
        quantise_wo(0, wo_a)
        blocks = [project_row_block(0, j, f"value{j}") for j in range(2)]
        hq[(1, 0)] = quantise("h1a", hb)
        for j in range(2):
            store_row_block(j, project_row_block(1, j, blocks[j]))
        quantise_wo(1, wo_b)
        for j in range(2, 4):
            store_row_block(j, project_row_block(1, j, project_row_block(0, j, f"value{j}")))
        project_values(14)
        project_values(15)
        hb_c = gate_values(1, 2 * CHUNK, CHUNK, offset=36864)
        banks_c = [project(0, 2 * CHUNK, CHUNK, pair, f"value{pair}") for pair in range(2)]
        hq[(0, HALF + CHUNK)] = quantise("h0c", hb_end, offset=8192)
        hq[(1, 2 * CHUNK)] = quantise("h1c", hb_c)
        for pair in range(2):
            project(1, 2 * CHUNK, CHUNK, pair, banks_c[pair])
        hb_d = gate_values(1, 3 * CHUNK, GROUP, offset=12288)
        banks_d = [project(0, 3 * CHUNK, GROUP, pair, f"value{2 + pair}") for pair in range(2)]
        banks_e = [project(0, 3 * CHUNK + GROUP, GROUP, pair, wide_banks[pair]) for pair in range(2)]
        hb_e = gate_values(1, 3 * CHUNK + GROUP, GROUP, offset=12288 + 1024)
        hq[(1, 3 * CHUNK)] = quantise("h1d", hb_d)
        for pair in range(2):
            project(1, 3 * CHUNK, GROUP, pair, banks_d[pair])
        hq[(1, 3 * CHUNK + GROUP)] = quantise("h1e", hb_e)
        for pair in range(2):
            project(1, 3 * CHUNK + GROUP, GROUP, pair, banks_e[pair])
        for pair in range(2):
            store(2 * CHUNK, CHUNK, pair, banks_c[pair])
        for i, banks in enumerate((banks_d, banks_e)):
            lo = 3 * CHUNK + GROUP * i
            res = held([P, N // P, GROUP], F32, f"res_last{i}")
            for pair in range(2):
                add_bias(res[:, 2 * pair : 2 * pair + 2, :], GROUP, pair, banks[pair], on_vector=(pair == 1))
            nc.sync.dma_start(out_rows[:, :, lo : lo + GROUP], res[:])
